import numpy as np
import ml_dtypes


def mxq(x, axis, fmt="e4m3"):
    dtype, down = {"e4m3": (ml_dtypes.float8_e4m3fn, 7), "e5m2": (ml_dtypes.float8_e5m2, 14)}[fmt]
    v = np.moveaxis(np.asarray(x, np.float32).astype(ml_dtypes.bfloat16).astype(np.float64), axis, -1)
    blocks = v.reshape(v.shape[:-1] + (-1, 32))
    amax = np.abs(blocks).max(-1, keepdims=True)
    byte = np.maximum(np.where(amax > 0, np.frexp(amax)[1] - 1 + 127, 0) - down, 1)
    scale = np.exp2(byte - 127.0)
    codes = (blocks / scale).astype(np.float32).astype(dtype).astype(np.float64)
    return np.moveaxis((codes * scale).reshape(v.shape), -1, axis)


WIDE = False


def mx_kscale(k):
    if not WIDE:
        return np.ones(k)
    levels = np.array([10, -10, 5, -5, 0])
    if k % 512:
        return np.exp2(np.random.permutation(np.resize(levels, k // 32))).repeat(32)
    a = np.empty((k // 512, 16))
    for p in range(k // 512):
        a[p, :8] = np.random.permutation(np.resize(levels, 8))
        for g in range(8):
            far = levels[np.abs(levels - a[p, g]) >= 10]
            a[p, g + 8] = far[np.random.randint(len(far))]
    return np.exp2(a.ravel()).repeat(32)


BF16 = ml_dtypes.bfloat16


def bf(x):
    return np.asarray(x, np.float32).astype(BF16)


def f64(x):
    return np.asarray(x).astype(np.float64)


N, D, K = 4096, 512, 512

DAMPING = 1.0


def softmax_rows(z):
    e = np.exp(z - z.max(axis=-1, keepdims=True))
    return e / e.sum(axis=-1, keepdims=True)


def softmax_hessian_product(p, jr, t):
    mu = np.sum(p * jr, axis=-1, keepdims=True)
    return t[:, None] * p * (jr - mu)


def draw0():
    s, a = mx_kscale(D), mx_kscale(N)
    x = np.random.standard_normal((N, D)) * s[None, :] * a[:, None]
    w = np.random.standard_normal((D, K)) * 2.0 / np.sqrt(D) / s[:, None]
    r = np.random.standard_normal((D, K)) * 0.25
    q = (1.0 + 0.1 * np.random.standard_normal(D)) / s
    t = (1.0 + 0.1 * np.random.standard_normal(N)) / a
    return {"x": bf(x), "w": bf(w), "r": bf(r), "q": bf(q), "t": bf(t)}


def core(x, w, r, q, t):
    x, w, r, q, t = f64(x), f64(w), f64(r), f64(q), f64(t)
    xd = mxq(x, 1, "e4m3")
    p = softmax_rows(t[:, None] * (xd @ mxq(w, 0, "e4m3")))
    v = q[:, None] * r
    jr = t[:, None] * (xd @ mxq(v, 0, "e4m3"))
    u = softmax_hessian_product(p, jr, t)
    ar = q[:, None] * (mxq(x, 0, "e4m3").T @ mxq(u, 0, "e4m3")) + DAMPING * r
    alpha = np.sum(r * r) / np.sum(r * ar)
    return r - alpha * ar


def e4m3fn_bytes(y):
    return np.clip(np.asarray(y, np.float64), -448.0, 448.0).astype(np.float32).astype(ml_dtypes.float8_e4m3fn).view(np.uint8)


def e4m3fn_values(b):
    return np.asarray(b, np.uint8).view(ml_dtypes.float8_e4m3fn).astype(np.float64)


def setup_inputs():
    d = draw0()
    x0 = np.asarray(d['w']).astype(np.float64)
    s = (np.max(np.abs(x0), axis=(1,), keepdims=True) / 448.0).astype(np.float32)
    out = {}
    for k, v in d.items():
        if k == 'w':
            out['w_bytes'] = e4m3fn_bytes(x0 / s.astype(np.float64))
            out['w_scale'] = s
        else:
            out[k] = v
    return out


def reference(x, w_bytes, w_scale, r, q, t):
    return core(x, e4m3fn_values(w_bytes) * w_scale.astype(np.float64), r, q, t)

@@ -1,0 +1,363 @@
+from contextlib import ExitStack
+
+import concourse.mybir as mybir
+from concourse.masks import make_identity
+
+N, D, K = 4096, 512, 512
+FLOPS = 3 * 2 * N * D * K
+
+F32 = mybir.dt.float32
+BF16 = mybir.dt.bfloat16
+U32 = mybir.dt.uint32
+U8 = mybir.dt.uint8
+FP8 = mybir.dt.float8_e4m3fn
+FP8X4 = mybir.dt.float8_e4m3fn_x4
+ALU = mybir.AluOpType
+ACT = mybir.ActivationFunctionType
+AX = mybir.AxisListType
+
+P = 128
+PACK = 4
+GROUP = P * PACK
+GROUPS = N // GROUP
+TILES = N // P
+QUARTER = K // 4
+
+
+def tile_gaussnewtonsoftmaxcgstep_t_kernel(tc, x, w_bytes, w_scale, r, q, t, out):
+    nc = tc.nc
+    with ExitStack() as ctx:
+        keep = ctx.enter_context(tc.tile_pool(name="keep", bufs=1))
+        two = ctx.enter_context(tc.tile_pool(name="two", bufs=2))
+        three = ctx.enter_context(tc.tile_pool(name="three", bufs=3))
+        psum = ctx.enter_context(tc.psum_pool(name="psum", bufs=1))
+        ctx.enter_context(tc.manual_schedule())
+
+        w_raw = keep.tile([P, PACK, K], U8, align_bytes=64)
+        w_sc = keep.tile([P, PACK], F32)
+        q_pj = keep.tile([P, PACK], BF16)
+        r_pj = keep.tile([P, PACK, K], BF16, align_bytes=64)
+        t_first = keep.tile([P, PACK], BF16)
+        t_rest = keep.tile([P, GROUPS - 1, PACK], BF16)
+        r_mp = keep.tile([P, PACK, K], BF16, align_bytes=64)
+        q_rows = keep.tile([P, P], BF16)
+        x_sb = {}
+
+        def load_x(g):
+            xt = keep.tile([P, PACK, D], BF16, tag=f"x{g}", align_bytes=64)
+            nc.sync.dma_start(out=xt[:], in_=x[g * GROUP : (g + 1) * GROUP, :].rearrange("(p j) d -> p j d", j=PACK))
+            x_sb[g] = xt
+
+        t_view = t.rearrange("(g p j) -> p g j", p=P, j=PACK)
+        nc.sync.dma_start(out=w_raw[:], in_=w_bytes.rearrange("(p j) n -> p j n", j=PACK))
+        nc.scalar.dma_start(out=w_sc[:], in_=w_scale.rearrange("(p j) o -> p (j o)", j=PACK))
+        load_x(0)
+        nc.scalar.dma_start(out=t_first[:], in_=t_view[:, 0, :])
+        nc.scalar.dma_start(out=q_pj[:], in_=q.rearrange("(p j) -> p j", j=PACK))
+        nc.gpsimd.memset(q_rows[:], 0.0)
+        nc.scalar.dma_start(out=q_rows[0:PACK, :], in_=q.rearrange("(m p) -> m p", p=P))
+        nc.sync.dma_start(out=r_pj[:], in_=r.rearrange("(p j) n -> p j n", j=PACK))
+        load_x(1)
+        nc.sync.dma_start(out=t_rest[:], in_=t_view[:, 1:GROUPS, :])
+        for g in range(2, GROUPS):
+            load_x(g)
+        nc.sync.dma_start(out=r_mp[:], in_=r.rearrange("(m p) n -> p m n", p=P))
+
+        ident = keep.tile([P, P], F32)
+        make_identity(nc, ident[:])
+        ones = keep.tile([P, P], F32)
+        nc.gpsimd.memset(ones[:], 1.0)
+        warm = keep.tile([P, 1], F32)
+        nc.vector.memset(warm[:], 0.0)
+        warm_out = keep.tile([P, 1], F32)
+        nc.scalar.activation(out=warm_out[:], in_=warm[:], func=ACT.Exp)
+
+        neg_t = keep.tile([P, TILES], F32)
+        t_sq = keep.tile([P, TILES], F32)
+        neg_max = keep.tile([P, TILES], F32)
+        exp_sum = keep.tile([P, TILES], F32)
+        inv_sum = keep.tile([P, TILES], F32)
+        coef = keep.tile([P, TILES], F32)
+        coef_inv = keep.tile([P, TILES], F32)
+        neg_dot = keep.tile([P, TILES], F32)
+        shift = keep.tile([P, TILES], F32)
+
+        xs_codes = keep.tile([P, GROUPS, D], U32, align_bytes=64)
+        xs_scales = keep.tile([P, GROUPS, D], U8, align_bytes=64)
+        u_codes = keep.tile([P, GROUPS, K], U32, align_bytes=64)
+        u_scales = keep.tile([P, GROUPS, K], U8, align_bytes=64)
+        w_codes = keep.tile([P, K], U32, align_bytes=64)
+        w_scales = keep.tile([P, K], U8, align_bytes=64)
+        v_codes = keep.tile([P, K], U32, align_bytes=64)
+        v_scales = keep.tile([P, K], U8, align_bytes=64)
+        w_b = keep.tile([P, PACK, K], BF16, align_bytes=64)
+        w_g = keep.tile([P, K, PACK], BF16, align_bytes=64)
+        v_b = keep.tile([P, PACK, K], BF16, align_bytes=64)
+        v_g = keep.tile([P, K, PACK], BF16, align_bytes=64)
+
+        t_bank, xt_g, xt_codes, xt_scales = {}, {}, {}, {}
+        xs_g, z_ps, z_sb, e_sb, j_ps, d_sb, u_g = {}, {}, {}, {}, {}, {}, {}
+
+        def by_rows(ap, i=4):
+            return ap.rearrange("p t (c i) -> p c t i", i=i)
+
+        def by_words(ap, i=4):
+            return ap.rearrange("p (c i) t -> p c t i", i=i)
+
+        def quantize(codes, scales, grouped):
+            nc.vector.quantize_mx(out=codes.bitcast(FP8X4), scales=scales, in_=grouped.rearrange("p n j -> p (n j)"))
+
+        def transposes(g):
+            words = x_sb[g][:].bitcast(F32)
+            for half in range(2):
+                bank = psum.tile([P, 2, 2, P], F32, tag=f"t{half}")
+                for jj in range(2):
+                    for u in range(2):
+                        nc.tensor.transpose(bank[:, jj, u, :], words[:, 2 * half + jj, u : D // 2 : 2], ident[:])
+                t_bank[g, half] = bank
+
+        def copy_transposed(g, half):
+            if half == 0:
+                grouped = two.tile([P, GROUP, PACK], BF16, tag="xt_g", align_bytes=64)
+                xt_g[g] = grouped
+            dst = xt_g[g][:, half * 256 : half * 256 + 256, :].bitcast(F32)
+            nc.scalar.copy(
+                out=dst.rearrange("p (j r) u -> p j r u", j=2),
+                in_=t_bank[g, half][:].rearrange("p j u r -> p j r u"),
+            )
+
+        def quantize_xt(g):
+            codes = two.tile([P, GROUP], U32, tag="xt_c", align_bytes=64)
+            scales = two.tile([P, GROUP], U8, tag="xt_s", align_bytes=64)
+            quantize(codes[:], scales[:], xt_g[g][:])
+            xt_codes[g], xt_scales[g] = codes, scales
+
+        def product(tag, i, codes, scales):
+            g, j = divmod(i, PACK)
+            cols = slice(j * P, j * P + P)
+            bank = psum.tile([P, K], F32, tag=tag)
+            nc.tensor.matmul_mx(
+                out=bank[:],
+                lhsT=xt_codes[g][:, cols].bitcast(FP8X4),
+                lhsT_scale=xt_scales[g][:, cols],
+                rhs=codes[:].bitcast(FP8X4),
+                rhs_scale=scales[:],
+                start=True,
+                stop=True,
+            )
+            return bank
+
+        def z_matmul(i):
+            z_ps[i] = product(f"z{i % 2}", i, w_codes, w_scales)
+
+        def j_matmul(i):
+            j_ps[i] = product(f"j{i % 2}", i, v_codes, v_scales)
+
+        def logits(i):
+            zt = three.tile([P, K], F32, tag="z")
+            nc.vector.tensor_scalar(
+                out=zt[:], in0=z_ps[i][:], scalar1=neg_t[:, i : i + 1], scalar2=None,
+                op0=ALU.mult, op1=ALU.min, accum_out=neg_max[:, i : i + 1],
+            )
+            z_sb[i] = zt
+
+        def exps(i):
+            g, j = divmod(i, PACK)
+            if j == 0:
+                et = three.tile([P, PACK, K], F32, tag="e")
+                e_sb[g] = et
+            nc.scalar.activation(
+                out=e_sb[g][:, j, :], in_=z_sb[i][:], func=ACT.Exp,
+                bias=neg_max[:, i : i + 1], scale=-1.0, accum_out=exp_sum[:, i : i + 1],
+            )
+
+        def coefs(i):
+            c = slice(i, i + 1)
+            nc.vector.reciprocal(out=inv_sum[:, c], in_=exp_sum[:, c])
+            nc.gpsimd.tensor_tensor(out=coef[:, c], in0=inv_sum[:, c], in1=t_sq[:, c], op=ALU.mult)
+            nc.gpsimd.tensor_tensor(out=coef_inv[:, c], in0=coef[:, c], in1=inv_sum[:, c], op=ALU.mult)
+
+        def dots(i):
+            g, j = divmod(i, PACK)
+            junk = two.tile([P, K], BF16, tag="junk")
+            nc.vector.scalar_tensor_tensor(
+                out=junk[:], in0=j_ps[i][:], scalar=-1.0, in1=e_sb[g][:, j, :],
+                op0=ALU.mult, op1=ALU.mult, accum_out=neg_dot[:, i : i + 1],
+            )
+
+        def shifts(i):
+            c = slice(i, i + 1)
+            nc.vector.tensor_tensor(out=shift[:, c], in0=neg_dot[:, c], in1=coef_inv[:, c], op=ALU.mult)
+
+        def centre(i):
+            g, j = divmod(i, PACK)
+            if j == 0:
+                dt = two.tile([P, PACK, K], F32, tag="d")
+                d_sb[g] = dt
+            nc.scalar.activation(
+                out=d_sb[g][:, j, :], in_=j_ps[i][:], func=ACT.Identity,
+                bias=shift[:, i : i + 1], scale=coef[:, i : i + 1],
+            )
+
+        def curvature(g, part, engine):
+            if part == 0:
+                ut = two.tile([P, K, PACK], BF16, tag="u_g", align_bytes=64)
+                u_g[g] = ut
+            cols = slice(part * QUARTER, (part + 1) * QUARTER)
+            engine.tensor_tensor(
+                out=by_words(u_g[g][:, cols, :]), in0=by_rows(d_sb[g][:, :, cols]), in1=by_rows(e_sb[g][:, :, cols]),
+                op=ALU.mult,
+            )
+
+        def quantize_u(g):
+            quantize(u_codes[:, g, :], u_scales[:, g, :], u_g[g][:])
+
+        def interleave_x(g, part):
+            if part == 0:
+                xg = two.tile([P, D, PACK], BF16, tag="xs_g", align_bytes=64)
+                xs_g[g] = xg
+            cols = slice(part * QUARTER, (part + 1) * QUARTER)
+            nc.scalar.copy(out=by_words(xs_g[g][:, cols, :]), in_=by_rows(x_sb[g][:, :, cols]))
+
+        def quantize_xs(g):
+            quantize(xs_codes[:, g, :], xs_scales[:, g, :], xs_g[g][:])
+
+        grad = {}
+
+        def grad_matmul(g, m):
+            if g == 0:
+                tag = f"t{m}" if m < 2 else f"g{m - 2}"
+                bank = psum.tile([P, K], F32, tag=tag)
+                grad[m] = bank
+            cols = slice(m * P, m * P + P)
+            nc.tensor.matmul_mx(
+                out=grad[m][:],
+                lhsT=xs_codes[:, g, cols].bitcast(FP8X4),
+                lhsT_scale=xs_scales[:, g, cols],
+                rhs=u_codes[:, g, :].bitcast(FP8X4),
+                rhs_scale=u_scales[:, g, :],
+                start=(g == 0),
+                stop=(g == GROUPS - 1),
+            )
+
+        for j in range(PACK):
+            if j < 2:
+                nc.vector.tensor_scalar(
+                    out=w_b[:, j, :], in0=w_raw[:, j, :].bitcast(FP8), scalar1=w_sc[:, j : j + 1], scalar2=None, op0=ALU.mult
+                )
+            else:
+                nc.scalar.activation(
+                    out=w_b[:, j, :], in_=w_raw[:, j, :].bitcast(FP8), func=ACT.Copy, scale=w_sc[:, j : j + 1]
+                )
+        transposes(0)
+        copy_transposed(0, 0)
+        copy_transposed(0, 1)
+        nc.vector.tensor_copy(out=by_words(w_g[:]), in_=by_rows(w_b[:]))
+        nc.vector.tensor_scalar(out=neg_t[:, 0:PACK], in0=t_first[:], scalar1=-1.0, scalar2=None, op0=ALU.mult)
+        nc.vector.tensor_tensor(out=t_sq[:, 0:PACK], in0=t_first[:], in1=t_first[:], op=ALU.mult)
+        quantize(w_codes[:], w_scales[:], w_g[:])
+        quantize_xt(0)
+        z_matmul(0)
+        z_matmul(1)
+        for j in range(PACK):
+            nc.vector.tensor_scalar(
+                out=v_b[:, j, :], in0=r_pj[:, j, :], scalar1=q_pj[:, j : j + 1], scalar2=None, op0=ALU.mult
+            )
+        logits(0)
+        exps(0)
+        nc.vector.tensor_copy(out=by_words(v_g[:]), in_=by_rows(v_b[:]))
+        coefs(0)
+        quantize(v_codes[:], v_scales[:], v_g[:])
+        j_matmul(0)
+        rest = t_rest[:].rearrange("p g j -> p (g j)")
+        nc.vector.tensor_scalar(out=neg_t[:, PACK:TILES], in0=rest, scalar1=-1.0, scalar2=None, op0=ALU.mult)
+        nc.vector.tensor_tensor(out=t_sq[:, PACK:TILES], in0=rest, in1=rest, op=ALU.mult)
+
+        q_wide = keep.tile([P, P], F32)
+        nc.gpsimd.tensor_copy(out=q_wide[:], in_=q_rows[:])
+        q_bank = psum.tile([P, P], F32, tag="g0")
+        nc.tensor.transpose(q_bank[:], q_wide[:], ident[:])
+        q_f = keep.tile([P, PACK], F32)
+        nc.vector.tensor_copy(out=q_f[:], in_=q_bank[:, 0:PACK])
+
+        for i in range(TILES):
+            g, j = divmod(i, PACK)
+            if i + 1 < TILES:
+                logits(i + 1)
+                exps(i + 1)
+            if j == 0 and g + 1 < GROUPS:
+                transposes(g + 1)
+            interleave_x(g, j)
+            if j < 2 and g + 1 < GROUPS:
+                copy_transposed(g + 1, j)
+            if g > 0:
+                curvature(g - 1, j, nc.vector)
+            if j == 0 and g > 1:
+                quantize_u(g - 2)
+            if j == 1 and g > 0:
+                quantize_xs(g - 1)
+            if j == 2 and g + 1 < GROUPS:
+                quantize_xt(g + 1)
+            dots(i)
+            if i + 1 < TILES:
+                coefs(i + 1)
+            shifts(i)
+            centre(i)
+            if i + 2 < TILES:
+                z_matmul(i + 2)
+            if i + 1 < TILES:
+                j_matmul(i + 1)
+            if j == 1 and g > 1:
+                grad_matmul(g - 2, 2)
+                grad_matmul(g - 2, 3)
+            if g == GROUPS - 1 and j >= 1:
+                for gg in range(2 * (j - 1), 2 * j):
+                    grad_matmul(gg, 0)
+                    grad_matmul(gg, 1)
+
+        last = GROUPS - 1
+        quantize_xs(last)
+        quantize_u(last - 1)
+        for m in range(PACK):
+            grad_matmul(last - 1, m)
+        for part in range(4):
+            curvature(last, part, nc.vector)
+        r_sq = keep.tile([P, 1], F32)
+        sums = keep.tile([P, PACK + 1], F32)
+        sq_junk = keep.tile([P, PACK * K], BF16)
+        nc.scalar.activation(
+            out=sq_junk[:], in_=r_mp[:].rearrange("p m n -> p (m n)"), func=ACT.Square, accum_out=r_sq[:]
+        )
+        quantize_u(last)
+        for m in range(PACK):
+            grad_matmul(last, m)
+        pair = keep.tile([P, 2], F32)
+        nc.vector.tensor_copy(out=sums[:, PACK : PACK + 1], in_=r_sq[:])
+        nc.vector.tensor_copy(out=pair[:, 1:2], in_=r_sq[:])
+        for m in range(PACK):
+            prod = two.tile([P, K], BF16, tag="junk")
+            nc.vector.scalar_tensor_tensor(
+                out=prod[:], in0=grad[m][:], scalar=q_f[:, m : m + 1], in1=r_mp[:, m, :],
+                op0=ALU.mult, op1=ALU.mult, accum_out=sums[:, m : m + 1],
+            )
+        nc.vector.tensor_reduce(out=pair[:, 0:1], in_=sums[:], axis=AX.X, op=ALU.add)
+        totals = psum.tile([P, 2], F32, tag="z0")
+        nc.tensor.matmul(totals[:], ones[:], pair[:], start=True, stop=True)
+        inv_den = keep.tile([P, 1], F32)
+        neg_alpha = keep.tile([P, 1], F32)
+        keep_r = keep.tile([P, 1], F32)
+        gain = keep.tile([P, PACK], F32)
+        nc.vector.reciprocal(out=inv_den[:], in_=totals[:, 0:1])
+        nc.vector.tensor_scalar(
+            out=neg_alpha[:], in0=totals[:, 1:2], scalar1=inv_den[:], scalar2=-1.0, op0=ALU.mult, op1=ALU.mult
+        )
+        nc.vector.tensor_scalar(out=keep_r[:], in0=neg_alpha[:], scalar1=1.0, scalar2=None, op0=ALU.add)
+        nc.vector.tensor_scalar(out=gain[:], in0=q_f[:], scalar1=neg_alpha[:], scalar2=None, op0=ALU.mult)
+        for m in range(PACK):
+            kept = two.tile([P, K], F32, tag="kept")
+            nc.scalar.activation(out=kept[:], in_=r_mp[:, m, :], func=ACT.Copy, scale=keep_r[:])
+            res = two.tile([P, K], F32, tag="res")
+            nc.vector.scalar_tensor_tensor(
+                out=res[:], in0=grad[m][:], scalar=gain[:, m : m + 1], in1=kept[:], op0=ALU.mult, op1=ALU.add
+            )
+            nc.sync.dma_start(out=out[m * P : (m + 1) * P, :], in_=res[:])

@@ -22,6 +22,7 @@ GROUP = P * PACK
 GROUPS = N // GROUP
 TILES = N // P
 QUARTER = K // 4
+PIECES = ((0,), (1,), (2,), (3,))
 
 
 def tile_gaussnewtonsoftmaxcgstep_t_kernel(tc, x, w_bytes, w_scale, r, q, t, out):
@@ -65,6 +66,8 @@ def tile_gaussnewtonsoftmaxcgstep_t_kernel(tc, x, w_bytes, w_scale, r, q, t, out
 
         ident = keep.tile([P, P], F32)
         make_identity(nc, ident[:])
+        ident_b = keep.tile([P, P], BF16)
+        nc.gpsimd.tensor_copy(out=ident_b[:], in_=ident[:])
         ones = keep.tile([P, P], F32)
         nc.gpsimd.memset(ones[:], 1.0)
         warm = keep.tile([P, 1], F32)
@@ -78,7 +81,6 @@ def tile_gaussnewtonsoftmaxcgstep_t_kernel(tc, x, w_bytes, w_scale, r, q, t, out
         exp_sum = keep.tile([P, TILES], F32)
         inv_sum = keep.tile([P, TILES], F32)
         coef = keep.tile([P, TILES], F32)
-        coef_inv = keep.tile([P, TILES], F32)
         neg_dot = keep.tile([P, TILES], F32)
         shift = keep.tile([P, TILES], F32)
 
@@ -107,14 +109,18 @@ def tile_gaussnewtonsoftmaxcgstep_t_kernel(tc, x, w_bytes, w_scale, r, q, t, out
         def quantize(codes, scales, grouped):
             nc.vector.quantize_mx(out=codes.bitcast(FP8X4), scales=scales, in_=grouped.rearrange("p n j -> p (n j)"))
 
-        def transposes(g):
-            words = x_sb[g][:].bitcast(F32)
-            for half in range(2):
+        def transpose_tile(g, j):
+            half, jj = divmod(j, 2)
+            if jj == 0:
                 bank = psum.tile([P, 2, 2, P], F32, tag=f"t{half}")
-                for jj in range(2):
-                    for u in range(2):
-                        nc.tensor.transpose(bank[:, jj, u, :], words[:, 2 * half + jj, u : D // 2 : 2], ident[:])
                 t_bank[g, half] = bank
+            words = x_sb[g][:, j, :].bitcast(F32)
+            for u in range(2):
+                nc.tensor.transpose(t_bank[g, half][:, jj, u, :], words[:, u : D // 2 : 2], ident[:])
+
+        def transposes(g):
+            for j in range(PACK):
+                transpose_tile(g, j)
 
         def copy_transposed(g, half):
             if half == 0:
@@ -126,11 +132,13 @@ def tile_gaussnewtonsoftmaxcgstep_t_kernel(tc, x, w_bytes, w_scale, r, q, t, out
                 in_=t_bank[g, half][:].rearrange("p j u r -> p j r u"),
             )
 
-        def quantize_xt(g):
-            codes = two.tile([P, GROUP], U32, tag="xt_c", align_bytes=64)
-            scales = two.tile([P, GROUP], U8, tag="xt_s", align_bytes=64)
-            quantize(codes[:], scales[:], xt_g[g][:])
-            xt_codes[g], xt_scales[g] = codes, scales
+        def quantize_xt(g, first=0, last=GROUP):
+            if first == 0:
+                codes = two.tile([P, GROUP], U32, tag="xt_c", align_bytes=64)
+                scales = two.tile([P, GROUP], U8, tag="xt_s", align_bytes=64)
+                xt_codes[g], xt_scales[g] = codes, scales
+            cols = slice(first, last)
+            quantize(xt_codes[g][:, cols], xt_scales[g][:, cols], xt_g[g][:, cols, :])
 
         def product(tag, i, codes, scales):
             g, j = divmod(i, PACK)
@@ -171,11 +179,13 @@ def tile_gaussnewtonsoftmaxcgstep_t_kernel(tc, x, w_bytes, w_scale, r, q, t, out
                 bias=neg_max[:, i : i + 1], scale=-1.0, accum_out=exp_sum[:, i : i + 1],
             )
 
-        def coefs(i):
+        def invert(i):
             c = slice(i, i + 1)
             nc.vector.reciprocal(out=inv_sum[:, c], in_=exp_sum[:, c])
-            nc.gpsimd.tensor_tensor(out=coef[:, c], in0=inv_sum[:, c], in1=t_sq[:, c], op=ALU.mult)
-            nc.gpsimd.tensor_tensor(out=coef_inv[:, c], in0=coef[:, c], in1=inv_sum[:, c], op=ALU.mult)
+
+        def coefs(i):
+            c = slice(i, i + 1)
+            nc.scalar.activation(out=coef[:, c], in_=inv_sum[:, c], func=ACT.Copy, scale=t_sq[:, c])
 
         def dots(i):
             g, j = divmod(i, PACK)
@@ -187,7 +197,9 @@ def tile_gaussnewtonsoftmaxcgstep_t_kernel(tc, x, w_bytes, w_scale, r, q, t, out
 
         def shifts(i):
             c = slice(i, i + 1)
-            nc.vector.tensor_tensor(out=shift[:, c], in0=neg_dot[:, c], in1=coef_inv[:, c], op=ALU.mult)
+            nc.vector.tensor_scalar(
+                out=shift[:, c], in0=neg_dot[:, c], scalar1=inv_sum[:, c], scalar2=coef[:, c], op0=ALU.mult, op1=ALU.mult
+            )
 
         def centre(i):
             g, j = divmod(i, PACK)
@@ -212,12 +224,33 @@ def tile_gaussnewtonsoftmaxcgstep_t_kernel(tc, x, w_bytes, w_scale, r, q, t, out
         def quantize_u(g):
             quantize(u_codes[:, g, :], u_scales[:, g, :], u_g[g][:])
 
-        def interleave_x(g, part):
-            if part == 0:
+        s_bank = {}
+
+        def interleave_part(g, part):
+            half, c = divmod(part, 2)
+            if c == 0:
+                bank = psum.tile([P, 2, GROUP], BF16, tag=f"g{half}")
+                s_bank[g, half] = bank
+            nc.tensor.matmul(
+                s_bank[g, half][:, c, :].rearrange("p (d j) -> p d j", j=PACK),
+                ident_b[:],
+                x_sb[g][:, :, part * P : part * P + P].rearrange("p j d -> p d j"),
+                start=True,
+                stop=True,
+            )
+
+        def interleave_x(g, half):
+            interleave_part(g, 2 * half)
+            interleave_part(g, 2 * half + 1)
+
+        def copy_interleaved(g, half):
+            if half == 0:
                 xg = two.tile([P, D, PACK], BF16, tag="xs_g", align_bytes=64)
                 xs_g[g] = xg
-            cols = slice(part * QUARTER, (part + 1) * QUARTER)
-            nc.scalar.copy(out=by_words(xs_g[g][:, cols, :]), in_=by_rows(x_sb[g][:, :, cols]))
+            nc.scalar.copy(
+                out=xs_g[g][:, half * 256 : half * 256 + 256, :].rearrange("p d j -> p (d j)"),
+                in_=s_bank[g, half][:].rearrange("p c n -> p (c n)"),
+            )
 
         def quantize_xs(g):
             quantize(xs_codes[:, g, :], xs_scales[:, g, :], xs_g[g][:])
@@ -256,68 +289,97 @@ def tile_gaussnewtonsoftmaxcgstep_t_kernel(tc, x, w_bytes, w_scale, r, q, t, out
         nc.vector.tensor_scalar(out=neg_t[:, 0:PACK], in0=t_first[:], scalar1=-1.0, scalar2=None, op0=ALU.mult)
         nc.vector.tensor_tensor(out=t_sq[:, 0:PACK], in0=t_first[:], in1=t_first[:], op=ALU.mult)
         quantize(w_codes[:], w_scales[:], w_g[:])
-        quantize_xt(0)
+        quantize_xt(0, 0, 256)
         z_matmul(0)
         z_matmul(1)
+        quantize_xt(0, 256, 512)
         for j in range(PACK):
             nc.vector.tensor_scalar(
                 out=v_b[:, j, :], in0=r_pj[:, j, :], scalar1=q_pj[:, j : j + 1], scalar2=None, op0=ALU.mult
             )
         logits(0)
+        z_matmul(2)
         exps(0)
         nc.vector.tensor_copy(out=by_words(v_g[:]), in_=by_rows(v_b[:]))
-        coefs(0)
+        transposes(1)
+        copy_transposed(1, 0)
+        copy_transposed(1, 1)
+        logits(1)
         quantize(v_codes[:], v_scales[:], v_g[:])
         j_matmul(0)
+        interleave_x(0, 0)
+        interleave_x(0, 1)
+        copy_interleaved(0, 0)
         rest = t_rest[:].rearrange("p g j -> p (g j)")
         nc.vector.tensor_scalar(out=neg_t[:, PACK:TILES], in0=rest, scalar1=-1.0, scalar2=None, op0=ALU.mult)
         nc.vector.tensor_tensor(out=t_sq[:, PACK:TILES], in0=rest, in1=rest, op=ALU.mult)
+        quantize_xt(1)
 
-        q_wide = keep.tile([P, P], F32)
-        nc.gpsimd.tensor_copy(out=q_wide[:], in_=q_rows[:])
-        q_bank = psum.tile([P, P], F32, tag="g0")
-        nc.tensor.transpose(q_bank[:], q_wide[:], ident[:])
-        q_f = keep.tile([P, PACK], F32)
-        nc.vector.tensor_copy(out=q_f[:], in_=q_bank[:, 0:PACK])
+        grad_plan = {}
+        for s in range(4):
+            grad_plan[20 + s] = [(s, 0), (s, 1)]
+        grad_plan[24] = [(4, 0), (4, 1)]
+        grad_plan[28] = [(0, 2), (0, 3), (1, 2), (1, 3)]
+        grad_plan[29] = [(2, 2), (2, 3), (3, 2), (3, 3)]
+        grad_plan[30] = [(5, 0), (5, 1), (4, 2), (4, 3)]
+        grad_plan[31] = [(5, 2), (5, 3)]
 
         for i in range(TILES):
             g, j = divmod(i, PACK)
+            window = j == PACK - 1
+            if i > 0:
+                centre(i - 1)
+            invert(i)
+            coefs(i)
             if i + 1 < TILES:
-                logits(i + 1)
                 exps(i + 1)
-            if j == 0 and g + 1 < GROUPS:
-                transposes(g + 1)
-            interleave_x(g, j)
-            if j < 2 and g + 1 < GROUPS:
-                copy_transposed(g + 1, j)
-            if g > 0:
-                curvature(g - 1, j, nc.vector)
-            if j == 0 and g > 1:
-                quantize_u(g - 2)
-            if j == 1 and g > 0:
-                quantize_xs(g - 1)
-            if j == 2 and g + 1 < GROUPS:
-                quantize_xt(g + 1)
+            if i == 0:
+                copy_interleaved(0, 1)
+            if j == 0 and g > 0:
+                for part in range(PACK):
+                    curvature(g - 1, part, nc.gpsimd)
             dots(i)
-            if i + 1 < TILES:
-                coefs(i + 1)
-            shifts(i)
-            centre(i)
             if i + 2 < TILES:
-                z_matmul(i + 2)
+                logits(i + 2)
+            if i + 3 < TILES:
+                z_matmul(i + 3)
             if i + 1 < TILES:
                 j_matmul(i + 1)
-            if j == 1 and g > 1:
-                grad_matmul(g - 2, 2)
-                grad_matmul(g - 2, 3)
-            if g == GROUPS - 1 and j >= 1:
-                for gg in range(2 * (j - 1), 2 * j):
-                    grad_matmul(gg, 0)
-                    grad_matmul(gg, 1)
+            if i == 0:
+                transposes(2)
+            if i == 1:
+                copy_transposed(2, 0)
+                copy_transposed(2, 1)
+            for part in PIECES[j]:
+                if g + 1 < GROUPS:
+                    interleave_part(g + 1, part)
+                if g + 3 < GROUPS:
+                    transpose_tile(g + 3, part)
+            if window:
+                if g > 0:
+                    quantize_u(g - 1)
+                quantize_xs(g)
+                if g + 2 < GROUPS:
+                    quantize_xt(g + 2)
+                for half in range(2):
+                    if g + 3 < GROUPS:
+                        copy_transposed(g + 3, half)
+                    if g + 1 < GROUPS:
+                        copy_interleaved(g + 1, half)
+            shifts(i)
+            if i == 2:
+                q_wide = keep.tile([P, P], F32)
+                nc.gpsimd.tensor_copy(out=q_wide[:], in_=q_rows[:])
+                q_bank = psum.tile([P, P], F32, tag="z0")
+                nc.tensor.transpose(q_bank[:], q_wide[:], ident[:])
+                q_f = keep.tile([P, PACK], F32)
+                nc.scalar.copy(out=q_f[:], in_=q_bank[:, 0:PACK])
+            if i in grad_plan:
+                for gg, m in grad_plan[i]:
+                    grad_matmul(gg, m)
 
         last = GROUPS - 1
-        quantize_xs(last)
-        quantize_u(last - 1)
+        centre(TILES - 1)
         for m in range(PACK):
             grad_matmul(last - 1, m)
         for part in range(4):

@@ -22,7 +22,8 @@ GROUP = P * PACK
 GROUPS = N // GROUP
 TILES = N // P
 QUARTER = K // 4
-PIECES = ((0,), (1,), (2,), (3,))
+SPLIT = 320
+LEAD = 4
 
 
 def tile_gaussnewtonsoftmaxcgstep_t_kernel(tc, x, w_bytes, w_scale, r, q, t, out):
@@ -81,6 +82,7 @@ def tile_gaussnewtonsoftmaxcgstep_t_kernel(tc, x, w_bytes, w_scale, r, q, t, out
         exp_sum = keep.tile([P, TILES], F32)
         inv_sum = keep.tile([P, TILES], F32)
         coef = keep.tile([P, TILES], F32)
+        coef_inv = keep.tile([P, TILES], F32)
         neg_dot = keep.tile([P, TILES], F32)
         shift = keep.tile([P, TILES], F32)
 
@@ -134,8 +136,8 @@ def tile_gaussnewtonsoftmaxcgstep_t_kernel(tc, x, w_bytes, w_scale, r, q, t, out
 
         def quantize_xt(g, first=0, last=GROUP):
             if first == 0:
-                codes = two.tile([P, GROUP], U32, tag="xt_c", align_bytes=64)
-                scales = two.tile([P, GROUP], U8, tag="xt_s", align_bytes=64)
+                codes = three.tile([P, GROUP], U32, tag="xt_c", align_bytes=64)
+                scales = three.tile([P, GROUP], U8, tag="xt_s", align_bytes=64)
                 xt_codes[g], xt_scales[g] = codes, scales
             cols = slice(first, last)
             quantize(xt_codes[g][:, cols], xt_scales[g][:, cols], xt_g[g][:, cols, :])
@@ -159,10 +161,10 @@ def tile_gaussnewtonsoftmaxcgstep_t_kernel(tc, x, w_bytes, w_scale, r, q, t, out
             z_ps[i] = product(f"z{i % 2}", i, w_codes, w_scales)
 
         def j_matmul(i):
-            j_ps[i] = product(f"j{i % 2}", i, v_codes, v_scales)
+            j_ps[i] = product(f"j{i % 3}", i, v_codes, v_scales)
 
         def logits(i):
-            zt = three.tile([P, K], F32, tag="z")
+            zt = three.tile([P, K], F32, tag="z", bufs=4)
             nc.vector.tensor_scalar(
                 out=zt[:], in0=z_ps[i][:], scalar1=neg_t[:, i : i + 1], scalar2=None,
                 op0=ALU.mult, op1=ALU.min, accum_out=neg_max[:, i : i + 1],
@@ -179,13 +181,11 @@ def tile_gaussnewtonsoftmaxcgstep_t_kernel(tc, x, w_bytes, w_scale, r, q, t, out
                 bias=neg_max[:, i : i + 1], scale=-1.0, accum_out=exp_sum[:, i : i + 1],
             )
 
-        def invert(i):
-            c = slice(i, i + 1)
+        def coefs(g):
+            c = slice(g * PACK, g * PACK + PACK)
             nc.vector.reciprocal(out=inv_sum[:, c], in_=exp_sum[:, c])
-
-        def coefs(i):
-            c = slice(i, i + 1)
-            nc.scalar.activation(out=coef[:, c], in_=inv_sum[:, c], func=ACT.Copy, scale=t_sq[:, c])
+            nc.gpsimd.tensor_tensor(out=coef[:, c], in0=inv_sum[:, c], in1=t_sq[:, c], op=ALU.mult)
+            nc.gpsimd.tensor_tensor(out=coef_inv[:, c], in0=inv_sum[:, c], in1=coef[:, c], op=ALU.mult)
 
         def dots(i):
             g, j = divmod(i, PACK)
@@ -197,9 +197,7 @@ def tile_gaussnewtonsoftmaxcgstep_t_kernel(tc, x, w_bytes, w_scale, r, q, t, out
 
         def shifts(i):
             c = slice(i, i + 1)
-            nc.vector.tensor_scalar(
-                out=shift[:, c], in0=neg_dot[:, c], scalar1=inv_sum[:, c], scalar2=coef[:, c], op0=ALU.mult, op1=ALU.mult
-            )
+            nc.scalar.activation(out=shift[:, c], in_=neg_dot[:, c], func=ACT.Copy, scale=coef_inv[:, c])
 
         def centre(i):
             g, j = divmod(i, PACK)
@@ -229,7 +227,7 @@ def tile_gaussnewtonsoftmaxcgstep_t_kernel(tc, x, w_bytes, w_scale, r, q, t, out
         def interleave_part(g, part):
             half, c = divmod(part, 2)
             if c == 0:
-                bank = psum.tile([P, 2, GROUP], BF16, tag=f"g{half}")
+                bank = psum.tile([P, 2, GROUP], BF16, tag="s")
                 s_bank[g, half] = bank
             nc.tensor.matmul(
                 s_bank[g, half][:, c, :].rearrange("p (d j) -> p d j", j=PACK),
@@ -238,10 +236,6 @@ def tile_gaussnewtonsoftmaxcgstep_t_kernel(tc, x, w_bytes, w_scale, r, q, t, out
                 start=True,
                 stop=True,
             )
-
-        def interleave_x(g, half):
-            interleave_part(g, 2 * half)
-            interleave_part(g, 2 * half + 1)
 
         def copy_interleaved(g, half):
             if half == 0:
@@ -259,7 +253,7 @@ def tile_gaussnewtonsoftmaxcgstep_t_kernel(tc, x, w_bytes, w_scale, r, q, t, out
 
         def grad_matmul(g, m):
             if g == 0:
-                tag = f"t{m}" if m < 2 else f"g{m - 2}"
+                tag = f"t{m}" if m < 2 else f"z{m - 2}"
                 bank = psum.tile([P, K], F32, tag=tag)
                 grad[m] = bank
             cols = slice(m * P, m * P + P)
@@ -273,8 +267,16 @@ def tile_gaussnewtonsoftmaxcgstep_t_kernel(tc, x, w_bytes, w_scale, r, q, t, out
                 stop=(g == GROUPS - 1),
             )
 
+        def t_columns(src, cols):
+            nc.gpsimd.tensor_scalar(out=neg_t[:, cols], in0=src, scalar1=-1.0, scalar2=0.0, op0=ALU.mult, op1=ALU.add)
+            nc.gpsimd.tensor_tensor(out=t_sq[:, cols], in0=src, in1=src, op=ALU.mult)
+
+        def interleave_split(dst, src):
+            for engine_copy, cols in ((nc.scalar.copy, slice(SPLIT, K)), (nc.vector.tensor_copy, slice(0, SPLIT))):
+                engine_copy(out=by_words(dst[:, cols, :]), in_=by_rows(src[:, :, cols]))
+
         for j in range(PACK):
-            if j < 2:
+            if j < 3:
                 nc.vector.tensor_scalar(
                     out=w_b[:, j, :], in0=w_raw[:, j, :].bitcast(FP8), scalar1=w_sc[:, j : j + 1], scalar2=None, op0=ALU.mult
                 )
@@ -282,144 +284,181 @@ def tile_gaussnewtonsoftmaxcgstep_t_kernel(tc, x, w_bytes, w_scale, r, q, t, out
                 nc.scalar.activation(
                     out=w_b[:, j, :], in_=w_raw[:, j, :].bitcast(FP8), func=ACT.Copy, scale=w_sc[:, j : j + 1]
                 )
+        t_columns(t_first[:], slice(0, PACK))
+        q_col = keep.tile([P, PACK], F32)
+        nc.gpsimd.tensor_copy(out=q_col[:], in_=q_pj[:])
+        interleave_split(w_g, w_b)
         transposes(0)
         copy_transposed(0, 0)
         copy_transposed(0, 1)
-        nc.vector.tensor_copy(out=by_words(w_g[:]), in_=by_rows(w_b[:]))
-        nc.vector.tensor_scalar(out=neg_t[:, 0:PACK], in0=t_first[:], scalar1=-1.0, scalar2=None, op0=ALU.mult)
-        nc.vector.tensor_tensor(out=t_sq[:, 0:PACK], in0=t_first[:], in1=t_first[:], op=ALU.mult)
         quantize(w_codes[:], w_scales[:], w_g[:])
         quantize_xt(0, 0, 256)
         z_matmul(0)
         z_matmul(1)
+        q_wide = keep.tile([P, P], F32)
+        nc.gpsimd.tensor_copy(out=q_wide[:], in_=q_rows[:])
+        q_bank = psum.tile([P, P], F32, tag="j2")
+        nc.tensor.transpose(q_bank[:], q_wide[:], ident[:])
+        q_f = keep.tile([P, PACK], F32)
+        nc.scalar.copy(out=q_f[:], in_=q_bank[:, 0:PACK])
+        transposes(1)
         quantize_xt(0, 256, 512)
-        for j in range(PACK):
+        logits(0)
+        z_matmul(2)
+        for j in range(2):
             nc.vector.tensor_scalar(
                 out=v_b[:, j, :], in0=r_pj[:, j, :], scalar1=q_pj[:, j : j + 1], scalar2=None, op0=ALU.mult
             )
-        logits(0)
-        z_matmul(2)
+        for j in range(2, PACK):
+            nc.scalar.activation(out=v_b[:, j, :], in_=r_pj[:, j, :], func=ACT.Copy, scale=q_col[:, j : j + 1])
         exps(0)
-        nc.vector.tensor_copy(out=by_words(v_g[:]), in_=by_rows(v_b[:]))
-        transposes(1)
+        logits(1)
+        z_matmul(3)
+        interleave_split(v_g, v_b)
+        t_columns(t_rest[:].rearrange("p g j -> p (g j)"), slice(PACK, TILES))
         copy_transposed(1, 0)
         copy_transposed(1, 1)
-        logits(1)
+        exps(1)
         quantize(v_codes[:], v_scales[:], v_g[:])
         j_matmul(0)
-        interleave_x(0, 0)
-        interleave_x(0, 1)
-        copy_interleaved(0, 0)
-        rest = t_rest[:].rearrange("p g j -> p (g j)")
-        nc.vector.tensor_scalar(out=neg_t[:, PACK:TILES], in0=rest, scalar1=-1.0, scalar2=None, op0=ALU.mult)
-        nc.vector.tensor_tensor(out=t_sq[:, PACK:TILES], in0=rest, in1=rest, op=ALU.mult)
+        transposes(2)
+        logits(2)
+        exps(2)
+        logits(3)
         quantize_xt(1)
+        z_matmul(4)
+        copy_transposed(2, 0)
+        copy_transposed(2, 1)
+        transposes(3)
+        interleave_part(0, 0)
+        interleave_part(0, 1)
 
         grad_plan = {}
         for s in range(4):
             grad_plan[20 + s] = [(s, 0), (s, 1)]
         grad_plan[24] = [(4, 0), (4, 1)]
-        grad_plan[28] = [(0, 2), (0, 3), (1, 2), (1, 3)]
-        grad_plan[29] = [(2, 2), (2, 3), (3, 2), (3, 3)]
-        grad_plan[30] = [(5, 0), (5, 1), (4, 2), (4, 3)]
-        grad_plan[31] = [(5, 2), (5, 3)]
+        grad_plan[31] = [(s, m) for s in range(5) for m in (2, 3)]
+        half_steps = [0, 3, 4, 7, 8, 11, 12, 15, 16, 19, 20, 21, 23, 24, 25, 27]
+        last = GROUPS - 1
+
+        def half_parts(i):
+            parts = []
+            for k in range(1, 2 * GROUPS):
+                lo, hi = half_steps[k - 1], half_steps[k]
+                for c in range(2):
+                    if i == min(lo + c, hi - 1):
+                        parts.append(2 * k + c)
+            return parts
 
         for i in range(TILES):
             g, j = divmod(i, PACK)
-            window = j == PACK - 1
+            if i > 0:
+                shifts(i - 1)
+            if i + LEAD - 1 < TILES:
+                exps(i + LEAD - 1)
             if i > 0:
                 centre(i - 1)
-            invert(i)
-            coefs(i)
-            if i + 1 < TILES:
-                exps(i + 1)
-            if i == 0:
-                copy_interleaved(0, 1)
-            if j == 0 and g > 0:
-                for part in range(PACK):
-                    curvature(g - 1, part, nc.gpsimd)
+            if j > 0 and i in half_steps:
+                copy_interleaved(*divmod(half_steps.index(i), 2))
             dots(i)
-            if i + 2 < TILES:
-                logits(i + 2)
-            if i + 3 < TILES:
-                z_matmul(i + 3)
+            if i + LEAD < TILES:
+                logits(i + LEAD)
             if i + 1 < TILES:
                 j_matmul(i + 1)
-            if i == 0:
-                transposes(2)
-            if i == 1:
-                copy_transposed(2, 0)
-                copy_transposed(2, 1)
-            for part in PIECES[j]:
-                if g + 1 < GROUPS:
-                    interleave_part(g + 1, part)
-                if g + 3 < GROUPS:
-                    transpose_tile(g + 3, part)
-            if window:
+            if i + LEAD + 1 < TILES:
+                z_matmul(i + LEAD + 1)
+            if j == 0:
+                if 1 < g < last:
+                    quantize_u(g - 2)
                 if g > 0:
-                    quantize_u(g - 1)
-                quantize_xs(g)
+                    quantize_xs(g - 1)
                 if g + 2 < GROUPS:
                     quantize_xt(g + 2)
-                for half in range(2):
-                    if g + 3 < GROUPS:
-                        copy_transposed(g + 3, half)
-                    if g + 1 < GROUPS:
-                        copy_interleaved(g + 1, half)
-            shifts(i)
-            if i == 2:
-                q_wide = keep.tile([P, P], F32)
-                nc.gpsimd.tensor_copy(out=q_wide[:], in_=q_rows[:])
-                q_bank = psum.tile([P, P], F32, tag="z0")
-                nc.tensor.transpose(q_bank[:], q_wide[:], ident[:])
-                q_f = keep.tile([P, PACK], F32)
-                nc.scalar.copy(out=q_f[:], in_=q_bank[:, 0:PACK])
+                coefs(g)
+                if i in half_steps:
+                    copy_interleaved(*divmod(half_steps.index(i), 2))
+                if g + 3 < GROUPS:
+                    copy_transposed(g + 3, 0)
+                    copy_transposed(g + 3, 1)
+                if g > 0:
+                    for part in range(PACK if g < last else 2):
+                        curvature(g - 1, part, nc.gpsimd)
+            else:
+                if g + 4 < GROUPS:
+                    if j == 1:
+                        transpose_tile(g + 4, 0)
+                    if j == 2:
+                        transpose_tile(g + 4, 1)
+                    if j == 3:
+                        transpose_tile(g + 4, 2)
+                        transpose_tile(g + 4, 3)
+            for part in half_parts(i):
+                interleave_part(*divmod(part, PACK))
             if i in grad_plan:
                 for gg, m in grad_plan[i]:
                     grad_matmul(gg, m)
 
-        last = GROUPS - 1
+        shifts(TILES - 1)
         centre(TILES - 1)
+        quantize_u(last - 2)
+        for m in range(PACK):
+            grad_matmul(last - 2, m)
+        for part in range(2, PACK):
+            curvature(last - 1, part, nc.vector)
+        quantize_xs(last)
+        quantize_u(last - 1)
         for m in range(PACK):
             grad_matmul(last - 1, m)
-        for part in range(4):
+        for part in range(PACK):
             curvature(last, part, nc.vector)
         r_sq = keep.tile([P, 1], F32)
-        sums = keep.tile([P, PACK + 1], F32)
+        sums = keep.tile([P, PACK], F32)
         sq_junk = keep.tile([P, PACK * K], BF16)
         nc.scalar.activation(
             out=sq_junk[:], in_=r_mp[:].rearrange("p m n -> p (m n)"), func=ACT.Square, accum_out=r_sq[:]
         )
+        den = psum.tile([P, 1], F32, tag="j0")
+        num = psum.tile([P, 1], F32, tag="j1")
+        nc.tensor.matmul(num[:], ones[:], r_sq[:], start=True, stop=True)
+        nc.tensor.matmul(den[:], ones[:], r_sq[:], start=True, stop=False)
+        neg_num = keep.tile([P, 1], F32)
+        nc.scalar.activation(out=neg_num[:], in_=num[:], func=ACT.Copy, scale=-1.0)
         quantize_u(last)
         for m in range(PACK):
             grad_matmul(last, m)
-        pair = keep.tile([P, 2], F32)
-        nc.vector.tensor_copy(out=sums[:, PACK : PACK + 1], in_=r_sq[:])
-        nc.vector.tensor_copy(out=pair[:, 1:2], in_=r_sq[:])
         for m in range(PACK):
             prod = two.tile([P, K], BF16, tag="junk")
             nc.vector.scalar_tensor_tensor(
                 out=prod[:], in0=grad[m][:], scalar=q_f[:, m : m + 1], in1=r_mp[:, m, :],
                 op0=ALU.mult, op1=ALU.mult, accum_out=sums[:, m : m + 1],
             )
-        nc.vector.tensor_reduce(out=pair[:, 0:1], in_=sums[:], axis=AX.X, op=ALU.add)
-        totals = psum.tile([P, 2], F32, tag="z0")
-        nc.tensor.matmul(totals[:], ones[:], pair[:], start=True, stop=True)
+            nc.tensor.matmul(den[:], ones[:], sums[:, m : m + 1], start=False, stop=(m == PACK - 1))
+        applied = keep.tile([P, K], F32)
+        nc.vector.scalar_tensor_tensor(
+            out=applied[:], in0=grad[0][:], scalar=q_f[:, 0:1], in1=r_mp[:, 0, :], op0=ALU.mult, op1=ALU.add
+        )
         inv_den = keep.tile([P, 1], F32)
         neg_alpha = keep.tile([P, 1], F32)
         keep_r = keep.tile([P, 1], F32)
         gain = keep.tile([P, PACK], F32)
-        nc.vector.reciprocal(out=inv_den[:], in_=totals[:, 0:1])
+        nc.vector.reciprocal(out=inv_den[:], in_=den[:])
         nc.vector.tensor_scalar(
-            out=neg_alpha[:], in0=totals[:, 1:2], scalar1=inv_den[:], scalar2=-1.0, op0=ALU.mult, op1=ALU.mult
+            out=keep_r[:], in0=neg_num[:], scalar1=inv_den[:], scalar2=1.0, op0=ALU.mult, op1=ALU.add
         )
-        nc.vector.tensor_scalar(out=keep_r[:], in0=neg_alpha[:], scalar1=1.0, scalar2=None, op0=ALU.add)
-        nc.vector.tensor_scalar(out=gain[:], in0=q_f[:], scalar1=neg_alpha[:], scalar2=None, op0=ALU.mult)
+        nc.vector.tensor_scalar(out=neg_alpha[:], in0=neg_num[:], scalar1=inv_den[:], scalar2=None, op0=ALU.mult)
+        nc.vector.tensor_scalar(
+            out=gain[:], in0=q_f[:], scalar1=inv_den[:], scalar2=neg_num[:], op0=ALU.mult, op1=ALU.mult
+        )
         for m in range(PACK):
-            kept = two.tile([P, K], F32, tag="kept")
-            nc.scalar.activation(out=kept[:], in_=r_mp[:, m, :], func=ACT.Copy, scale=keep_r[:])
-            res = two.tile([P, K], F32, tag="res")
-            nc.vector.scalar_tensor_tensor(
-                out=res[:], in0=grad[m][:], scalar=gain[:, m : m + 1], in1=kept[:], op0=ALU.mult, op1=ALU.add
-            )
+            res = two.tile([P, K], F32, tag="res", bufs=4)
+            if m == 0:
+                nc.vector.scalar_tensor_tensor(
+                    out=res[:], in0=applied[:], scalar=neg_alpha[:], in1=r_mp[:, m, :], op0=ALU.mult, op1=ALU.add
+                )
+            else:
+                kept = two.tile([P, K], F32, tag="kept")
+                nc.scalar.activation(out=kept[:], in_=r_mp[:, m, :], func=ACT.Copy, scale=keep_r[:])
+                nc.vector.scalar_tensor_tensor(
+                    out=res[:], in0=grad[m][:], scalar=gain[:, m : m + 1], in1=kept[:], op0=ALU.mult, op1=ALU.add
+                )
             nc.sync.dma_start(out=out[m * P : (m + 1) * P, :], in_=res[:])

@@ -24,6 +24,12 @@ TILES = N // P
 QUARTER = K // 4
 SPLIT = 320
 LEAD = 4
+ENDPLAN = [(28, 0, "G"), (32, 1, "V"), (32, 2, "V"), (32, 3, "V")]
+QXS = 32
+C_STEPS = [k // 2 * 4 + k % 2 * 3 for k in range(16)]
+A_STEPS = [1, 3, 4, 6, 8, 10, 12, 14, 16, 18]
+AP = ((1, 1), (1, 1))
+CP = ((0, 0), (2, 1))
 
 
 def tile_gaussnewtonsoftmaxcgstep_t_kernel(tc, x, w_bytes, w_scale, r, q, t, out):
@@ -86,10 +92,8 @@ def tile_gaussnewtonsoftmaxcgstep_t_kernel(tc, x, w_bytes, w_scale, r, q, t, out
         neg_dot = keep.tile([P, TILES], F32)
         shift = keep.tile([P, TILES], F32)
 
-        xs_codes = keep.tile([P, GROUPS, D], U32, align_bytes=64)
-        xs_scales = keep.tile([P, GROUPS, D], U8, align_bytes=64)
-        u_codes = keep.tile([P, GROUPS, K], U32, align_bytes=64)
-        u_scales = keep.tile([P, GROUPS, K], U8, align_bytes=64)
+        xu_codes = keep.tile([P, GROUPS, 2, K], U32, align_bytes=64)
+        xu_scales = keep.tile([P, GROUPS, 2, K], U8, align_bytes=64)
         w_codes = keep.tile([P, K], U32, align_bytes=64)
         w_scales = keep.tile([P, K], U8, align_bytes=64)
         v_codes = keep.tile([P, K], U32, align_bytes=64)
@@ -100,7 +104,7 @@ def tile_gaussnewtonsoftmaxcgstep_t_kernel(tc, x, w_bytes, w_scale, r, q, t, out
         v_g = keep.tile([P, K, PACK], BF16, align_bytes=64)
 
         t_bank, xt_g, xt_codes, xt_scales = {}, {}, {}, {}
-        xs_g, z_ps, z_sb, e_sb, j_ps, d_sb, u_g = {}, {}, {}, {}, {}, {}, {}
+        z_ps, z_sb, e_sb, j_ps, d_sb, xu_g = {}, {}, {}, {}, {}, {}
 
         def by_rows(ap, i=4):
             return ap.rearrange("p t (c i) -> p c t i", i=i)
@@ -114,7 +118,7 @@ def tile_gaussnewtonsoftmaxcgstep_t_kernel(tc, x, w_bytes, w_scale, r, q, t, out
         def transpose_tile(g, j):
             half, jj = divmod(j, 2)
             if jj == 0:
-                bank = psum.tile([P, 2, 2, P], F32, tag=f"t{half}")
+                bank = psum.tile([P, 2, 2, P], F32, tag="j3" if half and g < 3 else "t")
                 t_bank[g, half] = bank
             words = x_sb[g][:, j, :].bitcast(F32)
             for u in range(2):
@@ -161,10 +165,10 @@ def tile_gaussnewtonsoftmaxcgstep_t_kernel(tc, x, w_bytes, w_scale, r, q, t, out
             z_ps[i] = product(f"z{i % 2}", i, w_codes, w_scales)
 
         def j_matmul(i):
-            j_ps[i] = product(f"j{i % 3}", i, v_codes, v_scales)
+            j_ps[i] = product(f"j{i % 4}", i, v_codes, v_scales)
 
         def logits(i):
-            zt = three.tile([P, K], F32, tag="z", bufs=4)
+            zt = three.tile([P, K], F32, tag="z", bufs=6)
             nc.vector.tensor_scalar(
                 out=zt[:], in0=z_ps[i][:], scalar1=neg_t[:, i : i + 1], scalar2=None,
                 op0=ALU.mult, op1=ALU.min, accum_out=neg_max[:, i : i + 1],
@@ -210,17 +214,21 @@ def tile_gaussnewtonsoftmaxcgstep_t_kernel(tc, x, w_bytes, w_scale, r, q, t, out
             )
 
         def curvature(g, part, engine):
-            if part == 0:
-                ut = two.tile([P, K, PACK], BF16, tag="u_g", align_bytes=64)
-                u_g[g] = ut
             cols = slice(part * QUARTER, (part + 1) * QUARTER)
             engine.tensor_tensor(
-                out=by_words(u_g[g][:, cols, :]), in0=by_rows(d_sb[g][:, :, cols]), in1=by_rows(e_sb[g][:, :, cols]),
+                out=by_words(xu_g[g][:, 1, cols, :]), in0=by_rows(d_sb[g][:, :, cols]), in1=by_rows(e_sb[g][:, :, cols]),
                 op=ALU.mult,
             )
 
-        def quantize_u(g):
-            quantize(u_codes[:, g, :], u_scales[:, g, :], u_g[g][:])
+        def quantize_xu(g):
+            nc.vector.quantize_mx(
+                out=xu_codes[:, g].rearrange("p h n -> p (h n)").bitcast(FP8X4),
+                scales=xu_scales[:, g].rearrange("p h n -> p (h n)"),
+                in_=xu_g[g][:].rearrange("p h n j -> p (h n j)"),
+            )
+
+        def quantize_half(g, h):
+            quantize(xu_codes[:, g, h, :], xu_scales[:, g, h, :], xu_g[g][:, h])
 
         s_bank = {}
 
@@ -239,30 +247,28 @@ def tile_gaussnewtonsoftmaxcgstep_t_kernel(tc, x, w_bytes, w_scale, r, q, t, out
 
         def copy_interleaved(g, half):
             if half == 0:
-                xg = two.tile([P, D, PACK], BF16, tag="xs_g", align_bytes=64)
-                xs_g[g] = xg
+                xg = three.tile([P, 2, K, PACK], BF16, tag="xu_g", align_bytes=64)
+                xu_g[g] = xg
             nc.scalar.copy(
-                out=xs_g[g][:, half * 256 : half * 256 + 256, :].rearrange("p d j -> p (d j)"),
+                out=xu_g[g][:, 0, half * 256 : half * 256 + 256, :].rearrange("p d j -> p (d j)"),
                 in_=s_bank[g, half][:].rearrange("p c n -> p (c n)"),
             )
 
-        def quantize_xs(g):
-            quantize(xs_codes[:, g, :], xs_scales[:, g, :], xs_g[g][:])
 
         grad = {}
 
         def grad_matmul(g, m):
             if g == 0:
-                tag = f"t{m}" if m < 2 else f"z{m - 2}"
+                tag = ("t", "s", "z0", "z1")[m]
                 bank = psum.tile([P, K], F32, tag=tag)
                 grad[m] = bank
             cols = slice(m * P, m * P + P)
             nc.tensor.matmul_mx(
                 out=grad[m][:],
-                lhsT=xs_codes[:, g, cols].bitcast(FP8X4),
-                lhsT_scale=xs_scales[:, g, cols],
-                rhs=u_codes[:, g, :].bitcast(FP8X4),
-                rhs_scale=u_scales[:, g, :],
+                lhsT=xu_codes[:, g, 0, cols].bitcast(FP8X4),
+                lhsT_scale=xu_scales[:, g, 0, cols],
+                rhs=xu_codes[:, g, 1, :].bitcast(FP8X4),
+                rhs_scale=xu_scales[:, g, 1, :],
                 start=(g == 0),
                 stop=(g == GROUPS - 1),
             )
@@ -295,12 +301,6 @@ def tile_gaussnewtonsoftmaxcgstep_t_kernel(tc, x, w_bytes, w_scale, r, q, t, out
         quantize_xt(0, 0, 256)
         z_matmul(0)
         z_matmul(1)
-        q_wide = keep.tile([P, P], F32)
-        nc.gpsimd.tensor_copy(out=q_wide[:], in_=q_rows[:])
-        q_bank = psum.tile([P, P], F32, tag="j2")
-        nc.tensor.transpose(q_bank[:], q_wide[:], ident[:])
-        q_f = keep.tile([P, PACK], F32)
-        nc.scalar.copy(out=q_f[:], in_=q_bank[:, 0:PACK])
         transposes(1)
         quantize_xt(0, 256, 512)
         logits(0)
@@ -321,92 +321,94 @@ def tile_gaussnewtonsoftmaxcgstep_t_kernel(tc, x, w_bytes, w_scale, r, q, t, out
         exps(1)
         quantize(v_codes[:], v_scales[:], v_g[:])
         j_matmul(0)
+        j_matmul(1)
         transposes(2)
+        quantize_xt(1)
         logits(2)
+        z_matmul(4)
         exps(2)
         logits(3)
-        quantize_xt(1)
-        z_matmul(4)
+        z_matmul(5)
         copy_transposed(2, 0)
         copy_transposed(2, 1)
-        transposes(3)
+        q_wide = keep.tile([P, P], F32)
+        nc.gpsimd.tensor_copy(out=q_wide[:], in_=q_rows[:])
+        q_bank = psum.tile([P, P], F32, tag="s")
+        nc.tensor.transpose(q_bank[:], q_wide[:], ident[:])
+        q_f = keep.tile([P, PACK], F32)
+        nc.scalar.copy(out=q_f[:], in_=q_bank[:, 0:PACK])
         interleave_part(0, 0)
         interleave_part(0, 1)
 
-        grad_plan = {}
-        for s in range(4):
-            grad_plan[20 + s] = [(s, 0), (s, 1)]
-        grad_plan[24] = [(4, 0), (4, 1)]
-        grad_plan[31] = [(s, m) for s in range(5) for m in (2, 3)]
-        half_steps = [0, 3, 4, 7, 8, 11, 12, 15, 16, 19, 20, 21, 23, 24, 25, 27]
         last = GROUPS - 1
-
-        def half_parts(i):
-            parts = []
-            for k in range(1, 2 * GROUPS):
-                lo, hi = half_steps[k - 1], half_steps[k]
-                for c in range(2):
-                    if i == min(lo + c, hi - 1):
-                        parts.append(2 * k + c)
-            return parts
+        grad_plan = {i: [] for i in range(TILES)}
+        for s in range(4):
+            grad_plan[20 + s].append((s, 0))
+        grad_plan[24].append((4, 0))
+        grad_plan[28].append((5, 0))
+        grad_plan[30] += [(s, 2) for s in range(6)]
+        grad_plan[31] += [(s, m) for m in (3, 1) for s in range(6)]
+        copies = {i: [] for i in range(TILES)}
+        pieces = {i: [] for i in range(TILES)}
+        for k in range(2 * (GROUPS - 3)):
+            copies[A_STEPS[k]].append((1, 3 + k // 2, k % 2))
+            for c in range(2):
+                pieces[A_STEPS[k] - AP[k % 2][c]].append((1, 3 + k // 2, 2 * (k % 2) + c))
+        for k in range(2 * GROUPS):
+            copies[C_STEPS[k]].append((0, k // 2, k % 2))
+            for c in range(2 if k > 0 else 0):
+                pieces[C_STEPS[k] - CP[k % 2][c]].append((0, k // 2, 2 * (k % 2) + c))
 
         for i in range(TILES):
             g, j = divmod(i, PACK)
             if i > 0:
                 shifts(i - 1)
-            if i + LEAD - 1 < TILES:
-                exps(i + LEAD - 1)
+            for n in range(4 if i == 0 else i + LEAD, min(i + LEAD + 1, TILES)):
+                logits(n)
+            for n in range(3 if i == 0 else i + LEAD - 1, min(i + LEAD, TILES)):
+                exps(n)
             if i > 0:
                 centre(i - 1)
-            if j > 0 and i in half_steps:
-                copy_interleaved(*divmod(half_steps.index(i), 2))
             dots(i)
-            if i + LEAD < TILES:
-                logits(i + LEAD)
-            if i + 1 < TILES:
-                j_matmul(i + 1)
-            if i + LEAD + 1 < TILES:
-                z_matmul(i + LEAD + 1)
+            for n in range(6 if i == 0 else i + LEAD + 1, min(i + LEAD + 2, TILES)):
+                z_matmul(n)
+            if i + 2 < TILES:
+                j_matmul(i + 2)
             if j == 0:
-                if 1 < g < last:
-                    quantize_u(g - 2)
-                if g > 0:
-                    quantize_xs(g - 1)
+                if g > 1:
+                    quantize_xu(g - 2)
                 if g + 2 < GROUPS:
                     quantize_xt(g + 2)
                 coefs(g)
-                if i in half_steps:
-                    copy_interleaved(*divmod(half_steps.index(i), 2))
-                if g + 3 < GROUPS:
-                    copy_transposed(g + 3, 0)
-                    copy_transposed(g + 3, 1)
-                if g > 0:
-                    for part in range(PACK if g < last else 2):
+                if 0 < g < last:
+                    for part in range(PACK):
                         curvature(g - 1, part, nc.gpsimd)
-            else:
-                if g + 4 < GROUPS:
-                    if j == 1:
-                        transpose_tile(g + 4, 0)
-                    if j == 2:
-                        transpose_tile(g + 4, 1)
-                    if j == 3:
-                        transpose_tile(g + 4, 2)
-                        transpose_tile(g + 4, 3)
-            for part in half_parts(i):
-                interleave_part(*divmod(part, PACK))
-            if i in grad_plan:
-                for gg, m in grad_plan[i]:
-                    grad_matmul(gg, m)
+            for step, part, who in ENDPLAN:
+                if step == i:
+                    curvature(last - 1, part, nc.gpsimd if who == "G" else nc.vector)
+            for kind, cg, part in pieces[i]:
+                if kind == 0:
+                    interleave_part(cg, part)
+                else:
+                    transpose_tile(cg, part)
+            if i == QXS:
+                quantize_half(last, 0)
+            for kind, cg, half in copies[i]:
+                if kind == 0:
+                    copy_interleaved(cg, half)
+                else:
+                    copy_transposed(cg, half)
+            for gg, m in grad_plan[i]:
+                grad_matmul(gg, m)
 
         shifts(TILES - 1)
         centre(TILES - 1)
-        quantize_u(last - 2)
-        for m in range(PACK):
-            grad_matmul(last - 2, m)
-        for part in range(2, PACK):
-            curvature(last - 1, part, nc.vector)
-        quantize_xs(last)
-        quantize_u(last - 1)
+        for step, part, who in ENDPLAN:
+            if step == 32:
+                curvature(last - 1, part, nc.vector)
+        if QXS == 32:
+            quantize_half(last, 0)
+        quantize_xu(last - 1)
         for m in range(PACK):
             grad_matmul(last - 1, m)
         for part in range(PACK):
@@ -423,7 +425,7 @@ def tile_gaussnewtonsoftmaxcgstep_t_kernel(tc, x, w_bytes, w_scale, r, q, t, out
         nc.tensor.matmul(den[:], ones[:], r_sq[:], start=True, stop=False)
         neg_num = keep.tile([P, 1], F32)
         nc.scalar.activation(out=neg_num[:], in_=num[:], func=ACT.Copy, scale=-1.0)
-        quantize_u(last)
+        quantize_half(last, 1)
         for m in range(PACK):
             grad_matmul(last, m)
         for m in range(PACK):
@@ -442,10 +444,8 @@ def tile_gaussnewtonsoftmaxcgstep_t_kernel(tc, x, w_bytes, w_scale, r, q, t, out
         keep_r = keep.tile([P, 1], F32)
         gain = keep.tile([P, PACK], F32)
         nc.vector.reciprocal(out=inv_den[:], in_=den[:])
-        nc.vector.tensor_scalar(
-            out=keep_r[:], in0=neg_num[:], scalar1=inv_den[:], scalar2=1.0, op0=ALU.mult, op1=ALU.add
-        )
         nc.vector.tensor_scalar(out=neg_alpha[:], in0=neg_num[:], scalar1=inv_den[:], scalar2=None, op0=ALU.mult)
+        nc.scalar.activation(out=keep_r[:], in_=inv_den[:], func=ACT.Identity, scale=neg_num[:], bias=1.0)
         nc.vector.tensor_scalar(
             out=gain[:], in0=q_f[:], scalar1=inv_den[:], scalar2=neg_num[:], op0=ALU.mult, op1=ALU.mult
         )
@@ -458,7 +458,17 @@ def tile_gaussnewtonsoftmaxcgstep_t_kernel(tc, x, w_bytes, w_scale, r, q, t, out
             else:
                 kept = two.tile([P, K], F32, tag="kept")
                 nc.scalar.activation(out=kept[:], in_=r_mp[:, m, :], func=ACT.Copy, scale=keep_r[:])
-                nc.vector.scalar_tensor_tensor(
-                    out=res[:], in0=grad[m][:], scalar=gain[:, m : m + 1], in1=kept[:], op0=ALU.mult, op1=ALU.add
-                )
-            nc.sync.dma_start(out=out[m * P : (m + 1) * P, :], in_=res[:])
+                if m < PACK - 1:
+                    nc.vector.scalar_tensor_tensor(
+                        out=res[:], in0=grad[m][:], scalar=gain[:, m : m + 1], in1=kept[:], op0=ALU.mult, op1=ALU.add
+                    )
+            if m < PACK - 1:
+                nc.sync.dma_start(out=out[m * P : (m + 1) * P, :], in_=res[:])
+            else:
+                for c in range(2):
+                    cols = slice(c * K // 2, (c + 1) * K // 2)
+                    nc.vector.scalar_tensor_tensor(
+                        out=res[:, cols], in0=grad[m][:, cols], scalar=gain[:, m : m + 1], in1=kept[:, cols],
+                        op0=ALU.mult, op1=ALU.add,
+                    )
+                    nc.sync.dma_start(out=out[m * P : (m + 1) * P, cols], in_=res[:, cols])

@@ -14,22 +14,26 @@ FP8 = mybir.dt.float8_e4m3fn
 FP8X4 = mybir.dt.float8_e4m3fn_x4
 ALU = mybir.AluOpType
 ACT = mybir.ActivationFunctionType
-AX = mybir.AxisListType
 
 P = 128
 PACK = 4
 GROUP = P * PACK
 GROUPS = N // GROUP
+LAST = GROUPS - 1
 TILES = N // P
-QUARTER = K // 4
+HALF = GROUP // 2
+LEAD = 5
 SPLIT = 320
-LEAD = 4
-ENDPLAN = [(28, 0, "G"), (32, 1, "V"), (32, 2, "V"), (32, 3, "V")]
-QXS = 32
-C_STEPS = [k // 2 * 4 + k % 2 * 3 for k in range(16)]
-A_STEPS = [1, 3, 4, 6, 8, 10, 12, 14, 16, 18]
-AP = ((1, 1), (1, 1))
-CP = ((0, 0), (2, 1))
+VECTOR_COLS = 64
+FIRST_GRAD_TURN = 20
+
+
+def feature_turn(g, half):
+    return 1 + half if g == 3 else 4 * (g - 3) + 2 * half
+
+
+def due(i, ahead, start):
+    return range(start if i == 0 else i + ahead, min(i + ahead + 1, TILES))
 
 
 def tile_gaussnewtonsoftmaxcgstep_t_kernel(tc, x, w_bytes, w_scale, r, q, t, out):
@@ -44,17 +48,17 @@ def tile_gaussnewtonsoftmaxcgstep_t_kernel(tc, x, w_bytes, w_scale, r, q, t, out
         w_raw = keep.tile([P, PACK, K], U8, align_bytes=64)
         w_sc = keep.tile([P, PACK], F32)
         q_pj = keep.tile([P, PACK], BF16)
+        q_rows = keep.tile([P, P], BF16)
         r_pj = keep.tile([P, PACK, K], BF16, align_bytes=64)
+        r_mp = keep.tile([P, PACK, K], BF16, align_bytes=64)
         t_first = keep.tile([P, PACK], BF16)
         t_rest = keep.tile([P, GROUPS - 1, PACK], BF16)
-        r_mp = keep.tile([P, PACK, K], BF16, align_bytes=64)
-        q_rows = keep.tile([P, P], BF16)
         x_sb = {}
 
         def load_x(g):
-            xt = keep.tile([P, PACK, D], BF16, tag=f"x{g}", align_bytes=64)
-            nc.sync.dma_start(out=xt[:], in_=x[g * GROUP : (g + 1) * GROUP, :].rearrange("(p j) d -> p j d", j=PACK))
-            x_sb[g] = xt
+            rows = keep.tile([P, PACK, D], BF16, tag=f"x{g}", align_bytes=64)
+            nc.sync.dma_start(out=rows[:], in_=x[g * GROUP : (g + 1) * GROUP, :].rearrange("(p j) d -> p j d", j=PACK))
+            x_sb[g] = rows
 
         t_view = t.rearrange("(g p j) -> p g j", p=P, j=PACK)
         nc.sync.dma_start(out=w_raw[:], in_=w_bytes.rearrange("(p j) n -> p j n", j=PACK))
@@ -84,12 +88,13 @@ def tile_gaussnewtonsoftmaxcgstep_t_kernel(tc, x, w_bytes, w_scale, r, q, t, out
 
         neg_t = keep.tile([P, TILES], F32)
         t_sq = keep.tile([P, TILES], F32)
+        neg_t_sq = keep.tile([P, TILES], F32)
         neg_max = keep.tile([P, TILES], F32)
         exp_sum = keep.tile([P, TILES], F32)
         inv_sum = keep.tile([P, TILES], F32)
         coef = keep.tile([P, TILES], F32)
-        coef_inv = keep.tile([P, TILES], F32)
-        neg_dot = keep.tile([P, TILES], F32)
+        neg_coef = keep.tile([P, TILES], F32)
+        dot_scale = keep.tile([P, TILES], F32)
         shift = keep.tile([P, TILES], F32)
 
         xu_codes = keep.tile([P, GROUPS, 2, K], U32, align_bytes=64)
@@ -103,50 +108,70 @@ def tile_gaussnewtonsoftmaxcgstep_t_kernel(tc, x, w_bytes, w_scale, r, q, t, out
         v_b = keep.tile([P, PACK, K], BF16, align_bytes=64)
         v_g = keep.tile([P, K, PACK], BF16, align_bytes=64)
 
-        t_bank, xt_g, xt_codes, xt_scales = {}, {}, {}, {}
-        z_ps, z_sb, e_sb, j_ps, d_sb, xu_g = {}, {}, {}, {}, {}, {}
+        t_bank, s_bank, xt_g, xt_codes, xt_scales = {}, {}, {}, {}, {}
+        z_ps, z_sb, e_sb, j_ps, d_sb, xu_g, grad = {}, {}, {}, {}, {}, {}, {}
 
-        def by_rows(ap, i=4):
-            return ap.rearrange("p t (c i) -> p c t i", i=i)
+        def by_rows(ap):
+            return ap.rearrange("p j (c i) -> p c j i", i=4)
 
-        def by_words(ap, i=4):
-            return ap.rearrange("p (c i) t -> p c t i", i=i)
+        def by_words(ap):
+            return ap.rearrange("p (c i) j -> p c j i", i=4)
 
         def quantize(codes, scales, grouped):
             nc.vector.quantize_mx(out=codes.bitcast(FP8X4), scales=scales, in_=grouped.rearrange("p n j -> p (n j)"))
 
-        def transpose_tile(g, j):
-            half, jj = divmod(j, 2)
-            if jj == 0:
-                bank = psum.tile([P, 2, 2, P], F32, tag="j3" if half and g < 3 else "t")
-                t_bank[g, half] = bank
-            words = x_sb[g][:, j, :].bitcast(F32)
-            for u in range(2):
-                nc.tensor.transpose(t_bank[g, half][:, jj, u, :], words[:, u : D // 2 : 2], ident[:])
-
-        def transposes(g):
-            for j in range(PACK):
-                transpose_tile(g, j)
+        def transpose_half(g, half):
+            bank = psum.tile([P, 2, 2, P], F32, tag="j3" if half and g < 3 else "t")
+            for jj in range(2):
+                words = x_sb[g][:, 2 * half + jj, :].bitcast(F32)
+                for u in range(2):
+                    nc.tensor.transpose(bank[:, jj, u, :], words[:, u : D // 2 : 2], ident[:])
+            t_bank[g, half] = bank
 
         def copy_transposed(g, half):
             if half == 0:
                 grouped = two.tile([P, GROUP, PACK], BF16, tag="xt_g", align_bytes=64)
                 xt_g[g] = grouped
-            dst = xt_g[g][:, half * 256 : half * 256 + 256, :].bitcast(F32)
+            words = xt_g[g][:, half * HALF : half * HALF + HALF, :].bitcast(F32)
             nc.scalar.copy(
-                out=dst.rearrange("p (j r) u -> p j r u", j=2),
+                out=words.rearrange("p (j r) u -> p j r u", j=2),
                 in_=t_bank[g, half][:].rearrange("p j u r -> p j r u"),
             )
 
-        def quantize_xt(g, first=0, last=GROUP):
+        def quantize_xt(g, first=0, end=GROUP):
             if first == 0:
                 codes = three.tile([P, GROUP], U32, tag="xt_c", align_bytes=64)
                 scales = three.tile([P, GROUP], U8, tag="xt_s", align_bytes=64)
                 xt_codes[g], xt_scales[g] = codes, scales
-            cols = slice(first, last)
+            cols = slice(first, end)
             quantize(xt_codes[g][:, cols], xt_scales[g][:, cols], xt_g[g][:, cols, :])
 
-        def product(tag, i, codes, scales):
+        def interleave_quarter(g, quarter):
+            half, c = divmod(quarter, 2)
+            if c == 0:
+                bank = psum.tile([P, 2, GROUP], BF16, tag="s")
+                s_bank[g, half] = bank
+            nc.tensor.matmul(
+                s_bank[g, half][:, c, :].rearrange("p (d j) -> p d j", j=PACK),
+                ident_b[:],
+                x_sb[g][:, :, quarter * P : quarter * P + P].rearrange("p j d -> p d j"),
+                start=True,
+                stop=True,
+            )
+
+        def open_xu(g):
+            if g not in xu_g:
+                grouped = three.tile([P, 2, K, PACK], BF16, tag="xu_g", align_bytes=64)
+                xu_g[g] = grouped
+
+        def copy_interleaved(g, half):
+            open_xu(g)
+            nc.scalar.copy(
+                out=xu_g[g][:, 0, half * HALF : half * HALF + HALF, :].rearrange("p d j -> p (d j)"),
+                in_=s_bank[g, half][:].rearrange("p c n -> p (c n)"),
+            )
+
+        def product(i, tag, codes, scales):
             g, j = divmod(i, PACK)
             cols = slice(j * P, j * P + P)
             bank = psum.tile([P, K], F32, tag=tag)
@@ -162,61 +187,65 @@ def tile_gaussnewtonsoftmaxcgstep_t_kernel(tc, x, w_bytes, w_scale, r, q, t, out
             return bank
 
         def z_matmul(i):
-            z_ps[i] = product(f"z{i % 2}", i, w_codes, w_scales)
+            z_ps[i] = product(i, f"z{i % 2}", w_codes, w_scales)
 
         def j_matmul(i):
-            j_ps[i] = product(f"j{i % 4}", i, v_codes, v_scales)
+            j_ps[i] = product(i, f"j{i % 4}", v_codes, v_scales)
 
         def logits(i):
-            zt = three.tile([P, K], F32, tag="z", bufs=6)
+            c = slice(i, i + 1)
+            neg_z = three.tile([P, K], F32, tag="z", bufs=6)
             nc.vector.tensor_scalar(
-                out=zt[:], in0=z_ps[i][:], scalar1=neg_t[:, i : i + 1], scalar2=None,
-                op0=ALU.mult, op1=ALU.min, accum_out=neg_max[:, i : i + 1],
+                out=neg_z[:], in0=z_ps[i][:], scalar1=neg_t[:, c], scalar2=None,
+                op0=ALU.mult, op1=ALU.min, accum_out=neg_max[:, c],
             )
-            z_sb[i] = zt
+            z_sb[i] = neg_z
 
         def exps(i):
             g, j = divmod(i, PACK)
+            c = slice(i, i + 1)
             if j == 0:
-                et = three.tile([P, PACK, K], F32, tag="e")
-                e_sb[g] = et
+                e_group = three.tile([P, PACK, K], F32, tag="e")
+                e_sb[g] = e_group
             nc.scalar.activation(
-                out=e_sb[g][:, j, :], in_=z_sb[i][:], func=ACT.Exp,
-                bias=neg_max[:, i : i + 1], scale=-1.0, accum_out=exp_sum[:, i : i + 1],
+                out=e_sb[g][:, j, :], in_=z_sb[i][:], func=ACT.Exp, bias=neg_max[:, c], scale=-1.0, accum_out=exp_sum[:, c]
             )
+
+        def dot_scales(g):
+            c = slice(g * PACK, g * PACK + PACK)
+            nc.vector.reciprocal(out=inv_sum[:, c], in_=exp_sum[:, c])
+            nc.gpsimd.tensor_tensor(out=neg_coef[:, c], in0=inv_sum[:, c], in1=neg_t_sq[:, c], op=ALU.mult)
+            nc.gpsimd.tensor_tensor(out=dot_scale[:, c], in0=inv_sum[:, c], in1=neg_coef[:, c], op=ALU.mult)
 
         def coefs(g):
             c = slice(g * PACK, g * PACK + PACK)
-            nc.vector.reciprocal(out=inv_sum[:, c], in_=exp_sum[:, c])
             nc.gpsimd.tensor_tensor(out=coef[:, c], in0=inv_sum[:, c], in1=t_sq[:, c], op=ALU.mult)
-            nc.gpsimd.tensor_tensor(out=coef_inv[:, c], in0=inv_sum[:, c], in1=coef[:, c], op=ALU.mult)
 
         def dots(i):
             g, j = divmod(i, PACK)
-            junk = two.tile([P, K], BF16, tag="junk")
-            nc.vector.scalar_tensor_tensor(
-                out=junk[:], in0=j_ps[i][:], scalar=-1.0, in1=e_sb[g][:, j, :],
-                op0=ALU.mult, op1=ALU.mult, accum_out=neg_dot[:, i : i + 1],
-            )
-
-        def shifts(i):
             c = slice(i, i + 1)
-            nc.scalar.activation(out=shift[:, c], in_=neg_dot[:, c], func=ACT.Copy, scale=coef_inv[:, c])
+            unread = two.tile([P, K], BF16, tag="unread")
+            nc.vector.scalar_tensor_tensor(
+                out=unread[:], in0=j_ps[i][:], scalar=dot_scale[:, c], in1=e_sb[g][:, j, :],
+                op0=ALU.mult, op1=ALU.mult, accum_out=shift[:, c],
+            )
 
         def centre(i):
             g, j = divmod(i, PACK)
+            c = slice(i, i + 1)
             if j == 0:
-                dt = two.tile([P, PACK, K], F32, tag="d")
-                d_sb[g] = dt
+                d_group = two.tile([P, PACK, K], F32, tag="d")
+                d_sb[g] = d_group
             nc.scalar.activation(
-                out=d_sb[g][:, j, :], in_=j_ps[i][:], func=ACT.Identity,
-                bias=shift[:, i : i + 1], scale=coef[:, i : i + 1],
+                out=d_sb[g][:, j, :], in_=j_ps[i][:], func=ACT.Identity, bias=shift[:, c], scale=coef[:, c]
             )
 
-        def curvature(g, part, engine):
-            cols = slice(part * QUARTER, (part + 1) * QUARTER)
+        def curvature(g, first, end, engine):
+            open_xu(g)
             engine.tensor_tensor(
-                out=by_words(xu_g[g][:, 1, cols, :]), in0=by_rows(d_sb[g][:, :, cols]), in1=by_rows(e_sb[g][:, :, cols]),
+                out=by_words(xu_g[g][:, 1, first:end, :]),
+                in0=by_rows(d_sb[g][:, :, first:end]),
+                in1=by_rows(e_sb[g][:, :, first:end]),
                 op=ALU.mult,
             )
 
@@ -227,40 +256,12 @@ def tile_gaussnewtonsoftmaxcgstep_t_kernel(tc, x, w_bytes, w_scale, r, q, t, out
                 in_=xu_g[g][:].rearrange("p h n j -> p (h n j)"),
             )
 
-        def quantize_half(g, h):
+        def quantize_one(g, h):
             quantize(xu_codes[:, g, h, :], xu_scales[:, g, h, :], xu_g[g][:, h])
-
-        s_bank = {}
-
-        def interleave_part(g, part):
-            half, c = divmod(part, 2)
-            if c == 0:
-                bank = psum.tile([P, 2, GROUP], BF16, tag="s")
-                s_bank[g, half] = bank
-            nc.tensor.matmul(
-                s_bank[g, half][:, c, :].rearrange("p (d j) -> p d j", j=PACK),
-                ident_b[:],
-                x_sb[g][:, :, part * P : part * P + P].rearrange("p j d -> p d j"),
-                start=True,
-                stop=True,
-            )
-
-        def copy_interleaved(g, half):
-            if half == 0:
-                xg = three.tile([P, 2, K, PACK], BF16, tag="xu_g", align_bytes=64)
-                xu_g[g] = xg
-            nc.scalar.copy(
-                out=xu_g[g][:, 0, half * 256 : half * 256 + 256, :].rearrange("p d j -> p (d j)"),
-                in_=s_bank[g, half][:].rearrange("p c n -> p (c n)"),
-            )
-
-
-        grad = {}
 
         def grad_matmul(g, m):
             if g == 0:
-                tag = ("t", "s", "z0", "z1")[m]
-                bank = psum.tile([P, K], F32, tag=tag)
+                bank = psum.tile([P, K], F32, tag=("t", "s", "z0", "z1")[m])
                 grad[m] = bank
             cols = slice(m * P, m * P + P)
             nc.tensor.matmul_mx(
@@ -270,39 +271,41 @@ def tile_gaussnewtonsoftmaxcgstep_t_kernel(tc, x, w_bytes, w_scale, r, q, t, out
                 rhs=xu_codes[:, g, 1, :].bitcast(FP8X4),
                 rhs_scale=xu_scales[:, g, 1, :],
                 start=(g == 0),
-                stop=(g == GROUPS - 1),
+                stop=(g == LAST),
             )
 
         def t_columns(src, cols):
             nc.gpsimd.tensor_scalar(out=neg_t[:, cols], in0=src, scalar1=-1.0, scalar2=0.0, op0=ALU.mult, op1=ALU.add)
             nc.gpsimd.tensor_tensor(out=t_sq[:, cols], in0=src, in1=src, op=ALU.mult)
+            nc.gpsimd.tensor_tensor(out=neg_t_sq[:, cols], in0=src, in1=neg_t[:, cols], op=ALU.mult)
 
         def interleave_split(dst, src):
-            for engine_copy, cols in ((nc.scalar.copy, slice(SPLIT, K)), (nc.vector.tensor_copy, slice(0, SPLIT))):
-                engine_copy(out=by_words(dst[:, cols, :]), in_=by_rows(src[:, :, cols]))
+            nc.scalar.copy(out=by_words(dst[:, SPLIT:K, :]), in_=by_rows(src[:, :, SPLIT:K]))
+            nc.vector.tensor_copy(out=by_words(dst[:, 0:SPLIT, :]), in_=by_rows(src[:, :, 0:SPLIT]))
 
         for j in range(PACK):
+            w_row = w_raw[:, j, :].bitcast(FP8)
             if j < 3:
                 nc.vector.tensor_scalar(
-                    out=w_b[:, j, :], in0=w_raw[:, j, :].bitcast(FP8), scalar1=w_sc[:, j : j + 1], scalar2=None, op0=ALU.mult
+                    out=w_b[:, j, :], in0=w_row, scalar1=w_sc[:, j : j + 1], scalar2=None, op0=ALU.mult
                 )
             else:
-                nc.scalar.activation(
-                    out=w_b[:, j, :], in_=w_raw[:, j, :].bitcast(FP8), func=ACT.Copy, scale=w_sc[:, j : j + 1]
-                )
+                nc.scalar.activation(out=w_b[:, j, :], in_=w_row, func=ACT.Copy, scale=w_sc[:, j : j + 1])
         t_columns(t_first[:], slice(0, PACK))
         q_col = keep.tile([P, PACK], F32)
         nc.gpsimd.tensor_copy(out=q_col[:], in_=q_pj[:])
         interleave_split(w_g, w_b)
-        transposes(0)
-        copy_transposed(0, 0)
-        copy_transposed(0, 1)
+        for half in range(2):
+            transpose_half(0, half)
+        for half in range(2):
+            copy_transposed(0, half)
         quantize(w_codes[:], w_scales[:], w_g[:])
-        quantize_xt(0, 0, 256)
+        quantize_xt(0, 0, HALF)
         z_matmul(0)
         z_matmul(1)
-        transposes(1)
-        quantize_xt(0, 256, 512)
+        for half in range(2):
+            transpose_half(1, half)
+        quantize_xt(0, HALF, GROUP)
         logits(0)
         z_matmul(2)
         for j in range(2):
@@ -316,108 +319,106 @@ def tile_gaussnewtonsoftmaxcgstep_t_kernel(tc, x, w_bytes, w_scale, r, q, t, out
         z_matmul(3)
         interleave_split(v_g, v_b)
         t_columns(t_rest[:].rearrange("p g j -> p (g j)"), slice(PACK, TILES))
-        copy_transposed(1, 0)
-        copy_transposed(1, 1)
+        for half in range(2):
+            copy_transposed(1, half)
         exps(1)
         quantize(v_codes[:], v_scales[:], v_g[:])
         j_matmul(0)
         j_matmul(1)
-        transposes(2)
+        for half in range(2):
+            transpose_half(2, half)
         quantize_xt(1)
         logits(2)
         z_matmul(4)
         exps(2)
         logits(3)
+        exps(3)
         z_matmul(5)
-        copy_transposed(2, 0)
-        copy_transposed(2, 1)
+        for half in range(2):
+            copy_transposed(2, half)
         q_wide = keep.tile([P, P], F32)
         nc.gpsimd.tensor_copy(out=q_wide[:], in_=q_rows[:])
         q_bank = psum.tile([P, P], F32, tag="s")
         nc.tensor.transpose(q_bank[:], q_wide[:], ident[:])
-        q_f = keep.tile([P, PACK], F32)
-        nc.scalar.copy(out=q_f[:], in_=q_bank[:, 0:PACK])
-        interleave_part(0, 0)
-        interleave_part(0, 1)
+        q_mp = keep.tile([P, PACK], F32)
+        nc.scalar.copy(out=q_mp[:], in_=q_bank[:, 0:PACK])
+        for quarter in range(2):
+            interleave_quarter(0, quarter)
 
-        last = GROUPS - 1
-        grad_plan = {i: [] for i in range(TILES)}
-        for s in range(4):
-            grad_plan[20 + s].append((s, 0))
-        grad_plan[24].append((4, 0))
-        grad_plan[28].append((5, 0))
-        grad_plan[30] += [(s, 2) for s in range(6)]
-        grad_plan[31] += [(s, m) for m in (3, 1) for s in range(6)]
-        copies = {i: [] for i in range(TILES)}
-        pieces = {i: [] for i in range(TILES)}
-        for k in range(2 * (GROUPS - 3)):
-            copies[A_STEPS[k]].append((1, 3 + k // 2, k % 2))
-            for c in range(2):
-                pieces[A_STEPS[k] - AP[k % 2][c]].append((1, 3 + k // 2, 2 * (k % 2) + c))
-        for k in range(2 * GROUPS):
-            copies[C_STEPS[k]].append((0, k // 2, k % 2))
-            for c in range(2 if k > 0 else 0):
-                pieces[C_STEPS[k] - CP[k % 2][c]].append((0, k // 2, 2 * (k % 2) + c))
-
+        gpsimd_cols = (K - VECTOR_COLS) // PACK
         for i in range(TILES):
             g, j = divmod(i, PACK)
-            if i > 0:
-                shifts(i - 1)
-            for n in range(4 if i == 0 else i + LEAD, min(i + LEAD + 1, TILES)):
+            if j == 0:
+                if g > 1:
+                    curvature(g - 2, K - VECTOR_COLS, K, nc.vector)
+                if 0 < g < GROUPS - 2:
+                    quantize_xt(g + 2)
+                if g > 1:
+                    quantize_xu(g - 2)
+                dot_scales(g)
+            for n in due(i, LEAD, 4):
                 logits(n)
-            for n in range(3 if i == 0 else i + LEAD - 1, min(i + LEAD, TILES)):
-                exps(n)
             if i > 0:
                 centre(i - 1)
+            for n in due(i, LEAD - 1, 4):
+                exps(n)
             dots(i)
-            for n in range(6 if i == 0 else i + LEAD + 1, min(i + LEAD + 2, TILES)):
+            if i == 0:
+                quantize_xt(2)
+            for n in due(i, LEAD + 1, 6):
                 z_matmul(n)
             if i + 2 < TILES:
                 j_matmul(i + 2)
             if j == 0:
-                if g > 1:
-                    quantize_xu(g - 2)
-                if g + 2 < GROUPS:
-                    quantize_xt(g + 2)
-                coefs(g)
-                if 0 < g < last:
+                if 0 < g < LAST:
                     for part in range(PACK):
-                        curvature(g - 1, part, nc.gpsimd)
-            for step, part, who in ENDPLAN:
-                if step == i:
-                    curvature(last - 1, part, nc.gpsimd if who == "G" else nc.vector)
-            for kind, cg, part in pieces[i]:
-                if kind == 0:
-                    interleave_part(cg, part)
+                        curvature(g - 1, part * gpsimd_cols, (part + 1) * gpsimd_cols, nc.gpsimd)
+                        if part == 0:
+                            coefs(g)
                 else:
-                    transpose_tile(cg, part)
-            if i == QXS:
-                quantize_half(last, 0)
-            for kind, cg, half in copies[i]:
-                if kind == 0:
-                    copy_interleaved(cg, half)
-                else:
-                    copy_transposed(cg, half)
-            for gg, m in grad_plan[i]:
-                grad_matmul(gg, m)
+                    coefs(g)
+                if g == LAST:
+                    curvature(g - 1, 0, P, nc.gpsimd)
 
-        shifts(TILES - 1)
+            feature_halves = [(n, half) for n in range(3, GROUPS) for half in range(2)]
+            for n, half in feature_halves:
+                if feature_turn(n, half) == i + 1:
+                    transpose_half(n, half)
+            if j == 0 and g > 0:
+                interleave_quarter(g, 0)
+                interleave_quarter(g, 1)
+            if j == 1 or j == 2:
+                interleave_quarter(g, j + 1)
+            for n, half in feature_halves:
+                if feature_turn(n, half) == i:
+                    copy_transposed(n, half)
+            if j == 0:
+                copy_interleaved(g, 0)
+            if j == PACK - 1:
+                copy_interleaved(g, 1)
+
+            for n in range(LAST - 1):
+                if i == max(FIRST_GRAD_TURN + n, 4 * (n + 2)):
+                    grad_matmul(n, 0)
+            for m in {TILES - 2: (2,), TILES - 1: (3, 1)}.get(i, ()):
+                for n in range(LAST - 1):
+                    grad_matmul(n, m)
+
         centre(TILES - 1)
-        for step, part, who in ENDPLAN:
-            if step == 32:
-                curvature(last - 1, part, nc.vector)
-        if QXS == 32:
-            quantize_half(last, 0)
-        quantize_xu(last - 1)
+        for first in range(P, K, P):
+            curvature(LAST - 1, first, first + P, nc.vector)
+        quantize_one(LAST, 0)
+        quantize_xu(LAST - 1)
         for m in range(PACK):
-            grad_matmul(last - 1, m)
-        for part in range(PACK):
-            curvature(last, part, nc.vector)
+            grad_matmul(LAST - 1, m)
+        for first in range(0, K, P):
+            curvature(LAST, first, first + P, nc.vector)
+
         r_sq = keep.tile([P, 1], F32)
         sums = keep.tile([P, PACK], F32)
-        sq_junk = keep.tile([P, PACK * K], BF16)
+        squares = keep.tile([P, PACK * K], BF16)
         nc.scalar.activation(
-            out=sq_junk[:], in_=r_mp[:].rearrange("p m n -> p (m n)"), func=ACT.Square, accum_out=r_sq[:]
+            out=squares[:], in_=r_mp[:].rearrange("p m n -> p (m n)"), func=ACT.Square, accum_out=r_sq[:]
         )
         den = psum.tile([P, 1], F32, tag="j0")
         num = psum.tile([P, 1], F32, tag="j1")
@@ -425,19 +426,20 @@ def tile_gaussnewtonsoftmaxcgstep_t_kernel(tc, x, w_bytes, w_scale, r, q, t, out
         nc.tensor.matmul(den[:], ones[:], r_sq[:], start=True, stop=False)
         neg_num = keep.tile([P, 1], F32)
         nc.scalar.activation(out=neg_num[:], in_=num[:], func=ACT.Copy, scale=-1.0)
-        quantize_half(last, 1)
+        quantize_one(LAST, 1)
         for m in range(PACK):
-            grad_matmul(last, m)
+            grad_matmul(LAST, m)
         for m in range(PACK):
-            prod = two.tile([P, K], BF16, tag="junk")
+            unread = two.tile([P, K], BF16, tag="unread")
             nc.vector.scalar_tensor_tensor(
-                out=prod[:], in0=grad[m][:], scalar=q_f[:, m : m + 1], in1=r_mp[:, m, :],
+                out=unread[:], in0=grad[m][:], scalar=q_mp[:, m : m + 1], in1=r_mp[:, m, :],
                 op0=ALU.mult, op1=ALU.mult, accum_out=sums[:, m : m + 1],
             )
             nc.tensor.matmul(den[:], ones[:], sums[:, m : m + 1], start=False, stop=(m == PACK - 1))
-        applied = keep.tile([P, K], F32)
+
+        ar_first = keep.tile([P, K], F32)
         nc.vector.scalar_tensor_tensor(
-            out=applied[:], in0=grad[0][:], scalar=q_f[:, 0:1], in1=r_mp[:, 0, :], op0=ALU.mult, op1=ALU.add
+            out=ar_first[:], in0=grad[0][:], scalar=q_mp[:, 0:1], in1=r_mp[:, 0, :], op0=ALU.mult, op1=ALU.add
         )
         inv_den = keep.tile([P, 1], F32)
         neg_alpha = keep.tile([P, 1], F32)
@@ -447,28 +449,24 @@ def tile_gaussnewtonsoftmaxcgstep_t_kernel(tc, x, w_bytes, w_scale, r, q, t, out
         nc.vector.tensor_scalar(out=neg_alpha[:], in0=neg_num[:], scalar1=inv_den[:], scalar2=None, op0=ALU.mult)
         nc.scalar.activation(out=keep_r[:], in_=inv_den[:], func=ACT.Identity, scale=neg_num[:], bias=1.0)
         nc.vector.tensor_scalar(
-            out=gain[:], in0=q_f[:], scalar1=inv_den[:], scalar2=neg_num[:], op0=ALU.mult, op1=ALU.mult
+            out=gain[:], in0=q_mp[:], scalar1=inv_den[:], scalar2=neg_num[:], op0=ALU.mult, op1=ALU.mult
         )
         for m in range(PACK):
+            rows = slice(m * P, m * P + P)
             res = two.tile([P, K], F32, tag="res", bufs=4)
             if m == 0:
                 nc.vector.scalar_tensor_tensor(
-                    out=res[:], in0=applied[:], scalar=neg_alpha[:], in1=r_mp[:, m, :], op0=ALU.mult, op1=ALU.add
+                    out=res[:], in0=ar_first[:], scalar=neg_alpha[:], in1=r_mp[:, m, :], op0=ALU.mult, op1=ALU.add
                 )
+                nc.sync.dma_start(out=out[rows, :], in_=res[:])
             else:
                 kept = two.tile([P, K], F32, tag="kept")
                 nc.scalar.activation(out=kept[:], in_=r_mp[:, m, :], func=ACT.Copy, scale=keep_r[:])
-                if m < PACK - 1:
-                    nc.vector.scalar_tensor_tensor(
-                        out=res[:], in0=grad[m][:], scalar=gain[:, m : m + 1], in1=kept[:], op0=ALU.mult, op1=ALU.add
-                    )
-            if m < PACK - 1:
-                nc.sync.dma_start(out=out[m * P : (m + 1) * P, :], in_=res[:])
-            else:
-                for c in range(2):
-                    cols = slice(c * K // 2, (c + 1) * K // 2)
+                width = K // 2 if m == PACK - 1 else K
+                for first in range(0, K, width):
+                    cols = slice(first, first + width)
                     nc.vector.scalar_tensor_tensor(
                         out=res[:, cols], in0=grad[m][:, cols], scalar=gain[:, m : m + 1], in1=kept[:, cols],
                         op0=ALU.mult, op1=ALU.add,
                     )
-                    nc.sync.dma_start(out=out[m * P : (m + 1) * P, cols], in_=res[:, cols])
+                    nc.sync.dma_start(out=out[rows, cols], in_=res[:, cols])

from contextlib import ExitStack

import concourse.mybir as mybir
from concourse.masks import make_identity

N, D, K = 4096, 512, 512
FLOPS = 3 * 2 * N * D * K

F32 = mybir.dt.float32
BF16 = mybir.dt.bfloat16
U32 = mybir.dt.uint32
U8 = mybir.dt.uint8
FP8 = mybir.dt.float8_e4m3fn
FP8X4 = mybir.dt.float8_e4m3fn_x4
ALU = mybir.AluOpType
ACT = mybir.ActivationFunctionType

P = 128
PACK = 4
GROUP = P * PACK
GROUPS = N // GROUP
LAST = GROUPS - 1
TILES = N // P
HALF = GROUP // 2
LEAD = 5
SPLIT = 320
VECTOR_COLS = 64
FIRST_GRAD_TURN = 20


def feature_turn(g, half):
    return 1 + half if g == 3 else 4 * (g - 3) + 2 * half


def due(i, ahead, start):
    return range(start if i == 0 else i + ahead, min(i + ahead + 1, TILES))


def tile_gaussnewtonsoftmaxcgstep_t_kernel(tc, x, w_bytes, w_scale, r, q, t, out):
    nc = tc.nc
    with ExitStack() as ctx:
        keep = ctx.enter_context(tc.tile_pool(name="keep", bufs=1))
        two = ctx.enter_context(tc.tile_pool(name="two", bufs=2))
        three = ctx.enter_context(tc.tile_pool(name="three", bufs=3))
        psum = ctx.enter_context(tc.psum_pool(name="psum", bufs=1))
        ctx.enter_context(tc.manual_schedule())

        w_raw = keep.tile([P, PACK, K], U8, align_bytes=64)
        w_sc = keep.tile([P, PACK], F32)
        q_pj = keep.tile([P, PACK], BF16)
        q_rows = keep.tile([P, P], BF16)
        r_pj = keep.tile([P, PACK, K], BF16, align_bytes=64)
        r_mp = keep.tile([P, PACK, K], BF16, align_bytes=64)
        t_first = keep.tile([P, PACK], BF16)
        t_rest = keep.tile([P, GROUPS - 1, PACK], BF16)
        x_sb = {}

        def load_x(g):
            rows = keep.tile([P, PACK, D], BF16, tag=f"x{g}", align_bytes=64)
            nc.sync.dma_start(out=rows[:], in_=x[g * GROUP : (g + 1) * GROUP, :].rearrange("(p j) d -> p j d", j=PACK))
            x_sb[g] = rows

        t_view = t.rearrange("(g p j) -> p g j", p=P, j=PACK)
        nc.sync.dma_start(out=w_raw[:], in_=w_bytes.rearrange("(p j) n -> p j n", j=PACK))
        nc.scalar.dma_start(out=w_sc[:], in_=w_scale.rearrange("(p j) o -> p (j o)", j=PACK))
        load_x(0)
        nc.scalar.dma_start(out=t_first[:], in_=t_view[:, 0, :])
        nc.scalar.dma_start(out=q_pj[:], in_=q.rearrange("(p j) -> p j", j=PACK))
        nc.gpsimd.memset(q_rows[:], 0.0)
        nc.scalar.dma_start(out=q_rows[0:PACK, :], in_=q.rearrange("(m p) -> m p", p=P))
        nc.sync.dma_start(out=r_pj[:], in_=r.rearrange("(p j) n -> p j n", j=PACK))
        load_x(1)
        nc.sync.dma_start(out=t_rest[:], in_=t_view[:, 1:GROUPS, :])
        for g in range(2, GROUPS):
            load_x(g)
        nc.sync.dma_start(out=r_mp[:], in_=r.rearrange("(m p) n -> p m n", p=P))

        ident = keep.tile([P, P], F32)
        make_identity(nc, ident[:])
        ident_b = keep.tile([P, P], BF16)
        nc.gpsimd.tensor_copy(out=ident_b[:], in_=ident[:])
        ones = keep.tile([P, P], F32)
        nc.gpsimd.memset(ones[:], 1.0)
        warm = keep.tile([P, 1], F32)
        nc.vector.memset(warm[:], 0.0)
        warm_out = keep.tile([P, 1], F32)
        nc.scalar.activation(out=warm_out[:], in_=warm[:], func=ACT.Exp)

        neg_t = keep.tile([P, TILES], F32)
        t_sq = keep.tile([P, TILES], F32)
        neg_t_sq = keep.tile([P, TILES], F32)
        neg_max = keep.tile([P, TILES], F32)
        exp_sum = keep.tile([P, TILES], F32)
        inv_sum = keep.tile([P, TILES], F32)
        coef = keep.tile([P, TILES], F32)
        neg_coef = keep.tile([P, TILES], F32)
        dot_scale = keep.tile([P, TILES], F32)
        shift = keep.tile([P, TILES], F32)

        xu_codes = keep.tile([P, GROUPS, 2, K], U32, align_bytes=64)
        xu_scales = keep.tile([P, GROUPS, 2, K], U8, align_bytes=64)
        w_codes = keep.tile([P, K], U32, align_bytes=64)
        w_scales = keep.tile([P, K], U8, align_bytes=64)
        v_codes = keep.tile([P, K], U32, align_bytes=64)
        v_scales = keep.tile([P, K], U8, align_bytes=64)
        w_b = keep.tile([P, PACK, K], BF16, align_bytes=64)
        w_g = keep.tile([P, K, PACK], BF16, align_bytes=64)
        v_b = keep.tile([P, PACK, K], BF16, align_bytes=64)
        v_g = keep.tile([P, K, PACK], BF16, align_bytes=64)

        t_bank, s_bank, xt_g, xt_codes, xt_scales = {}, {}, {}, {}, {}
        z_ps, z_sb, e_sb, j_ps, d_sb, xu_g, grad = {}, {}, {}, {}, {}, {}, {}

        def by_rows(ap):
            return ap.rearrange("p j (c i) -> p c j i", i=4)

        def by_words(ap):
            return ap.rearrange("p (c i) j -> p c j i", i=4)

        def quantize(codes, scales, grouped):
            nc.vector.quantize_mx(out=codes.bitcast(FP8X4), scales=scales, in_=grouped.rearrange("p n j -> p (n j)"))

        def transpose_half(g, half):
            bank = psum.tile([P, 2, 2, P], F32, tag="j3" if half and g < 3 else "t")
            for jj in range(2):
                words = x_sb[g][:, 2 * half + jj, :].bitcast(F32)
                for u in range(2):
                    nc.tensor.transpose(bank[:, jj, u, :], words[:, u : D // 2 : 2], ident[:])
            t_bank[g, half] = bank

        def copy_transposed(g, half):
            if half == 0:
                grouped = two.tile([P, GROUP, PACK], BF16, tag="xt_g", align_bytes=64)
                xt_g[g] = grouped
            words = xt_g[g][:, half * HALF : half * HALF + HALF, :].bitcast(F32)
            nc.scalar.copy(
                out=words.rearrange("p (j r) u -> p j r u", j=2),
                in_=t_bank[g, half][:].rearrange("p j u r -> p j r u"),
            )

        def quantize_xt(g, first=0, end=GROUP):
            if first == 0:
                codes = three.tile([P, GROUP], U32, tag="xt_c", align_bytes=64)
                scales = three.tile([P, GROUP], U8, tag="xt_s", align_bytes=64)
                xt_codes[g], xt_scales[g] = codes, scales
            cols = slice(first, end)
            quantize(xt_codes[g][:, cols], xt_scales[g][:, cols], xt_g[g][:, cols, :])

        def interleave_quarter(g, quarter):
            half, c = divmod(quarter, 2)
            if c == 0:
                bank = psum.tile([P, 2, GROUP], BF16, tag="s")
                s_bank[g, half] = bank
            nc.tensor.matmul(
                s_bank[g, half][:, c, :].rearrange("p (d j) -> p d j", j=PACK),
                ident_b[:],
                x_sb[g][:, :, quarter * P : quarter * P + P].rearrange("p j d -> p d j"),
                start=True,
                stop=True,
            )

        def open_xu(g):
            if g not in xu_g:
                grouped = three.tile([P, 2, K, PACK], BF16, tag="xu_g", align_bytes=64)
                xu_g[g] = grouped

        def copy_interleaved(g, half):
            open_xu(g)
            nc.scalar.copy(
                out=xu_g[g][:, 0, half * HALF : half * HALF + HALF, :].rearrange("p d j -> p (d j)"),
                in_=s_bank[g, half][:].rearrange("p c n -> p (c n)"),
            )

        def product(i, tag, codes, scales):
            g, j = divmod(i, PACK)
            cols = slice(j * P, j * P + P)
            bank = psum.tile([P, K], F32, tag=tag)
            nc.tensor.matmul_mx(
                out=bank[:],
                lhsT=xt_codes[g][:, cols].bitcast(FP8X4),
                lhsT_scale=xt_scales[g][:, cols],
                rhs=codes[:].bitcast(FP8X4),
                rhs_scale=scales[:],
                start=True,
                stop=True,
            )
            return bank

        def z_matmul(i):
            z_ps[i] = product(i, f"z{i % 2}", w_codes, w_scales)

        def j_matmul(i):
            j_ps[i] = product(i, f"j{i % 4}", v_codes, v_scales)

        def logits(i):
            c = slice(i, i + 1)
            neg_z = three.tile([P, K], F32, tag="z", bufs=6)
            nc.vector.tensor_scalar(
                out=neg_z[:], in0=z_ps[i][:], scalar1=neg_t[:, c], scalar2=None,
                op0=ALU.mult, op1=ALU.min, accum_out=neg_max[:, c],
            )
            z_sb[i] = neg_z

        def exps(i):
            g, j = divmod(i, PACK)
            c = slice(i, i + 1)
            if j == 0:
                e_group = three.tile([P, PACK, K], F32, tag="e")
                e_sb[g] = e_group
            nc.scalar.activation(
                out=e_sb[g][:, j, :], in_=z_sb[i][:], func=ACT.Exp, bias=neg_max[:, c], scale=-1.0, accum_out=exp_sum[:, c]
            )

        def dot_scales(g):
            c = slice(g * PACK, g * PACK + PACK)
            nc.vector.reciprocal(out=inv_sum[:, c], in_=exp_sum[:, c])
            nc.gpsimd.tensor_tensor(out=neg_coef[:, c], in0=inv_sum[:, c], in1=neg_t_sq[:, c], op=ALU.mult)
            nc.gpsimd.tensor_tensor(out=dot_scale[:, c], in0=inv_sum[:, c], in1=neg_coef[:, c], op=ALU.mult)

        def coefs(g):
            c = slice(g * PACK, g * PACK + PACK)
            nc.gpsimd.tensor_tensor(out=coef[:, c], in0=inv_sum[:, c], in1=t_sq[:, c], op=ALU.mult)

        def dots(i):
            g, j = divmod(i, PACK)
            c = slice(i, i + 1)
            unread = two.tile([P, K], BF16, tag="unread")
            nc.vector.scalar_tensor_tensor(
                out=unread[:], in0=j_ps[i][:], scalar=dot_scale[:, c], in1=e_sb[g][:, j, :],
                op0=ALU.mult, op1=ALU.mult, accum_out=shift[:, c],
            )

        def centre(i):
            g, j = divmod(i, PACK)
            c = slice(i, i + 1)
            if j == 0:
                d_group = two.tile([P, PACK, K], F32, tag="d")
                d_sb[g] = d_group
            nc.scalar.activation(
                out=d_sb[g][:, j, :], in_=j_ps[i][:], func=ACT.Identity, bias=shift[:, c], scale=coef[:, c]
            )

        def curvature(g, first, end, engine):
            open_xu(g)
            engine.tensor_tensor(
                out=by_words(xu_g[g][:, 1, first:end, :]),
                in0=by_rows(d_sb[g][:, :, first:end]),
                in1=by_rows(e_sb[g][:, :, first:end]),
                op=ALU.mult,
            )

        def quantize_xu(g):
            nc.vector.quantize_mx(
                out=xu_codes[:, g].rearrange("p h n -> p (h n)").bitcast(FP8X4),
                scales=xu_scales[:, g].rearrange("p h n -> p (h n)"),
                in_=xu_g[g][:].rearrange("p h n j -> p (h n j)"),
            )

        def quantize_one(g, h):
            quantize(xu_codes[:, g, h, :], xu_scales[:, g, h, :], xu_g[g][:, h])

        def grad_matmul(g, m):
            if g == 0:
                bank = psum.tile([P, K], F32, tag=("t", "s", "z0", "z1")[m])
                grad[m] = bank
            cols = slice(m * P, m * P + P)
            nc.tensor.matmul_mx(
                out=grad[m][:],
                lhsT=xu_codes[:, g, 0, cols].bitcast(FP8X4),
                lhsT_scale=xu_scales[:, g, 0, cols],
                rhs=xu_codes[:, g, 1, :].bitcast(FP8X4),
                rhs_scale=xu_scales[:, g, 1, :],
                start=(g == 0),
                stop=(g == LAST),
            )

        def t_columns(src, cols):
            nc.gpsimd.tensor_scalar(out=neg_t[:, cols], in0=src, scalar1=-1.0, scalar2=0.0, op0=ALU.mult, op1=ALU.add)
            nc.gpsimd.tensor_tensor(out=t_sq[:, cols], in0=src, in1=src, op=ALU.mult)
            nc.gpsimd.tensor_tensor(out=neg_t_sq[:, cols], in0=src, in1=neg_t[:, cols], op=ALU.mult)

        def interleave_split(dst, src):
            nc.scalar.copy(out=by_words(dst[:, SPLIT:K, :]), in_=by_rows(src[:, :, SPLIT:K]))
            nc.vector.tensor_copy(out=by_words(dst[:, 0:SPLIT, :]), in_=by_rows(src[:, :, 0:SPLIT]))

        for j in range(PACK):
            w_row = w_raw[:, j, :].bitcast(FP8)
            if j < 3:
                nc.vector.tensor_scalar(
                    out=w_b[:, j, :], in0=w_row, scalar1=w_sc[:, j : j + 1], scalar2=None, op0=ALU.mult
                )
            else:
                nc.scalar.activation(out=w_b[:, j, :], in_=w_row, func=ACT.Copy, scale=w_sc[:, j : j + 1])
        t_columns(t_first[:], slice(0, PACK))
        q_col = keep.tile([P, PACK], F32)
        nc.gpsimd.tensor_copy(out=q_col[:], in_=q_pj[:])
        interleave_split(w_g, w_b)
        for half in range(2):
            transpose_half(0, half)
        for half in range(2):
            copy_transposed(0, half)
        quantize(w_codes[:], w_scales[:], w_g[:])
        quantize_xt(0, 0, HALF)
        z_matmul(0)
        z_matmul(1)
        for half in range(2):
            transpose_half(1, half)
        quantize_xt(0, HALF, GROUP)
        logits(0)
        z_matmul(2)
        for j in range(2):
            nc.vector.tensor_scalar(
                out=v_b[:, j, :], in0=r_pj[:, j, :], scalar1=q_pj[:, j : j + 1], scalar2=None, op0=ALU.mult
            )
        for j in range(2, PACK):
            nc.scalar.activation(out=v_b[:, j, :], in_=r_pj[:, j, :], func=ACT.Copy, scale=q_col[:, j : j + 1])
        exps(0)
        logits(1)
        z_matmul(3)
        interleave_split(v_g, v_b)
        t_columns(t_rest[:].rearrange("p g j -> p (g j)"), slice(PACK, TILES))
        for half in range(2):
            copy_transposed(1, half)
        exps(1)
        quantize(v_codes[:], v_scales[:], v_g[:])
        j_matmul(0)
        j_matmul(1)
        for half in range(2):
            transpose_half(2, half)
        quantize_xt(1)
        logits(2)
        z_matmul(4)
        exps(2)
        logits(3)
        exps(3)
        z_matmul(5)
        for half in range(2):
            copy_transposed(2, half)
        q_wide = keep.tile([P, P], F32)
        nc.gpsimd.tensor_copy(out=q_wide[:], in_=q_rows[:])
        q_bank = psum.tile([P, P], F32, tag="s")
        nc.tensor.transpose(q_bank[:], q_wide[:], ident[:])
        q_mp = keep.tile([P, PACK], F32)
        nc.scalar.copy(out=q_mp[:], in_=q_bank[:, 0:PACK])
        for quarter in range(2):
            interleave_quarter(0, quarter)

        gpsimd_cols = (K - VECTOR_COLS) // PACK
        for i in range(TILES):
            g, j = divmod(i, PACK)
            if j == 0:
                if g > 1:
                    curvature(g - 2, K - VECTOR_COLS, K, nc.vector)
                if 0 < g < GROUPS - 2:
                    quantize_xt(g + 2)
                if g > 1:
                    quantize_xu(g - 2)
                dot_scales(g)
            for n in due(i, LEAD, 4):
                logits(n)
            if i > 0:
                centre(i - 1)
            for n in due(i, LEAD - 1, 4):
                exps(n)
            dots(i)
            if i == 0:
                quantize_xt(2)
            for n in due(i, LEAD + 1, 6):
                z_matmul(n)
            if i + 2 < TILES:
                j_matmul(i + 2)
            if j == 0:
                if 0 < g < LAST:
                    for part in range(PACK):
                        curvature(g - 1, part * gpsimd_cols, (part + 1) * gpsimd_cols, nc.gpsimd)
                        if part == 0:
                            coefs(g)
                else:
                    coefs(g)
                if g == LAST:
                    curvature(g - 1, 0, P, nc.gpsimd)

            feature_halves = [(n, half) for n in range(3, GROUPS) for half in range(2)]
            for n, half in feature_halves:
                if feature_turn(n, half) == i + 1:
                    transpose_half(n, half)
            if j == 0 and g > 0:
                interleave_quarter(g, 0)
                interleave_quarter(g, 1)
            if j == 1 or j == 2:
                interleave_quarter(g, j + 1)
            for n, half in feature_halves:
                if feature_turn(n, half) == i:
                    copy_transposed(n, half)
            if j == 0:
                copy_interleaved(g, 0)
            if j == PACK - 1:
                copy_interleaved(g, 1)

            for n in range(LAST - 1):
                if i == max(FIRST_GRAD_TURN + n, 4 * (n + 2)):
                    grad_matmul(n, 0)
            for m in {TILES - 2: (2,), TILES - 1: (3, 1)}.get(i, ()):
                for n in range(LAST - 1):
                    grad_matmul(n, m)

        centre(TILES - 1)
        for first in range(P, K, P):
            curvature(LAST - 1, first, first + P, nc.vector)
        quantize_one(LAST, 0)
        quantize_xu(LAST - 1)
        for m in range(PACK):
            grad_matmul(LAST - 1, m)
        for first in range(0, K, P):
            curvature(LAST, first, first + P, nc.vector)

        r_sq = keep.tile([P, 1], F32)
        sums = keep.tile([P, PACK], F32)
        squares = keep.tile([P, PACK * K], BF16)
        nc.scalar.activation(
            out=squares[:], in_=r_mp[:].rearrange("p m n -> p (m n)"), func=ACT.Square, accum_out=r_sq[:]
        )
        den = psum.tile([P, 1], F32, tag="j0")
        num = psum.tile([P, 1], F32, tag="j1")
        nc.tensor.matmul(num[:], ones[:], r_sq[:], start=True, stop=True)
        nc.tensor.matmul(den[:], ones[:], r_sq[:], start=True, stop=False)
        neg_num = keep.tile([P, 1], F32)
        nc.scalar.activation(out=neg_num[:], in_=num[:], func=ACT.Copy, scale=-1.0)
        quantize_one(LAST, 1)
        for m in range(PACK):
            grad_matmul(LAST, m)
        for m in range(PACK):
            unread = two.tile([P, K], BF16, tag="unread")
            nc.vector.scalar_tensor_tensor(
                out=unread[:], in0=grad[m][:], scalar=q_mp[:, m : m + 1], in1=r_mp[:, m, :],
                op0=ALU.mult, op1=ALU.mult, accum_out=sums[:, m : m + 1],
            )
            nc.tensor.matmul(den[:], ones[:], sums[:, m : m + 1], start=False, stop=(m == PACK - 1))

        ar_first = keep.tile([P, K], F32)
        nc.vector.scalar_tensor_tensor(
            out=ar_first[:], in0=grad[0][:], scalar=q_mp[:, 0:1], in1=r_mp[:, 0, :], op0=ALU.mult, op1=ALU.add
        )
        inv_den = keep.tile([P, 1], F32)
        neg_alpha = keep.tile([P, 1], F32)
        keep_r = keep.tile([P, 1], F32)
        gain = keep.tile([P, PACK], F32)
        nc.vector.reciprocal(out=inv_den[:], in_=den[:])
        nc.vector.tensor_scalar(out=neg_alpha[:], in0=neg_num[:], scalar1=inv_den[:], scalar2=None, op0=ALU.mult)
        nc.scalar.activation(out=keep_r[:], in_=inv_den[:], func=ACT.Identity, scale=neg_num[:], bias=1.0)
        nc.vector.tensor_scalar(
            out=gain[:], in0=q_mp[:], scalar1=inv_den[:], scalar2=neg_num[:], op0=ALU.mult, op1=ALU.mult
        )
        for m in range(PACK):
            rows = slice(m * P, m * P + P)
            res = two.tile([P, K], F32, tag="res", bufs=4)
            if m == 0:
                nc.vector.scalar_tensor_tensor(
                    out=res[:], in0=ar_first[:], scalar=neg_alpha[:], in1=r_mp[:, m, :], op0=ALU.mult, op1=ALU.add
                )
                nc.sync.dma_start(out=out[rows, :], in_=res[:])
            else:
                kept = two.tile([P, K], F32, tag="kept")
                nc.scalar.activation(out=kept[:], in_=r_mp[:, m, :], func=ACT.Copy, scale=keep_r[:])
                width = K // 2 if m == PACK - 1 else K
                for first in range(0, K, width):
                    cols = slice(first, first + width)
                    nc.vector.scalar_tensor_tensor(
                        out=res[:, cols], in0=grad[m][:, cols], scalar=gain[:, m : m + 1], in1=kept[:, cols],
                        op0=ALU.mult, op1=ALU.add,
                    )
                    nc.sync.dma_start(out=out[rows, cols], in_=res[:, cols])
